import numpy as np
import ml_dtypes


def mxq(x, axis, fmt="e4m3"):
    dtype, down = {"e4m3": (ml_dtypes.float8_e4m3fn, 7), "e5m2": (ml_dtypes.float8_e5m2, 14)}[fmt]
    v = np.moveaxis(np.asarray(x, np.float32).astype(ml_dtypes.bfloat16).astype(np.float64), axis, -1)
    blocks = v.reshape(v.shape[:-1] + (-1, 32))
    amax = np.abs(blocks).max(-1, keepdims=True)
    byte = np.maximum(np.where(amax > 0, np.frexp(amax)[1] - 1 + 127, 0) - down, 1)
    scale = np.exp2(byte - 127.0)
    codes = (blocks / scale).astype(np.float32).astype(dtype).astype(np.float64)
    return np.moveaxis((codes * scale).reshape(v.shape), -1, axis)


WIDE = False


def mx_kscale(k):
    if not WIDE:
        return np.ones(k)
    levels = np.array([24, -24, 12, -12, 0])
    if k % 512:
        return np.exp2(np.random.permutation(np.resize(levels, k // 32))).repeat(32)
    a = np.empty((k // 512, 16))
    for p in range(k // 512):
        a[p, :8] = np.random.permutation(np.resize(levels, 8))
        for g in range(8):
            far = levels[np.abs(levels - a[p, g]) >= 10]
            a[p, g + 8] = far[np.random.randint(len(far))]
    return np.exp2(a.ravel()).repeat(32)


def f64(x):
    return np.asarray(x).astype(np.float64)


def striped(idx):
    return np.tile(idx.reshape(-1, 16).T, (8, 1)).astype(np.uint16)


def unstriped(offs):
    return offs[:16].T.reshape(-1).astype(np.int64)


E2M1 = np.array([0.0, 0.5, 1.0, 1.5, 2.0, 3.0, 4.0, 6.0, -0.0, -0.5, -1.0, -1.5, -2.0, -3.0, -4.0, -6.0])


def pack_weight(w, fmt):
    k, n = w.shape
    w = f64(np.asarray(w, np.float32).astype(ml_dtypes.bfloat16)).reshape(k // 32, 32, n)
    amax = np.abs(w).max(1)
    if fmt == "e4m3":
        byte = np.frexp(amax)[1] - 1 + 127 - 7
    else:
        mant, ex = np.frexp(amax / 6.0)
        byte = np.where(mant > 0.5, ex, ex - 1) + 127
    byte = np.clip(np.where(amax > 0, byte, 1), 1, 254)
    scaled = (w * np.exp2(127.0 - byte)[:, None, :]).reshape(k, n).astype(np.float32)
    by_word = np.ascontiguousarray(scaled.reshape(k // 512, 128, 4, n).transpose(0, 1, 3, 2))
    if fmt == "e4m3":
        words = by_word.astype(ml_dtypes.float8_e4m3fn).view(np.uint8)
    else:
        c = by_word.astype(ml_dtypes.float4_e2m1fn).view(np.uint8) & 0xF
        words = (c[..., 0::2] | (c[..., 1::2] << 4)).reshape(k // 512, 128, 2 * n)
    return np.ascontiguousarray(words), np.ascontiguousarray(byte.astype(np.uint8).reshape(k // 512, 16, n))


def unpack_weight(words, scales, fmt):
    g, _, n = scales.shape
    words = np.ascontiguousarray(words).reshape(g, 128, n, -1)
    if fmt == "e4m3":
        vals = words.view(ml_dtypes.float8_e4m3fn).astype(np.float64)
    else:
        nib = np.empty((g, 128, n, 4), np.uint8)
        nib[..., 0::2] = words & 0xF
        nib[..., 1::2] = words >> 4
        vals = E2M1[nib]
    vals = vals * np.repeat(np.exp2(scales.astype(np.float64) - 127.0), 8, axis=1)[..., None]
    return vals.transpose(0, 1, 3, 2).reshape(g * 512, n)


def pack_table4(v):
    words, scales = pack_weight(v, "e2m1")
    g, t = words.shape[0] // 2, v.shape[1]
    return np.ascontiguousarray(words.reshape(g, 2, 128, t, 2).transpose(0, 2, 3, 1, 4).reshape(g, 128, t, 4)), scales


def unpack_table4(words, scales):
    g, _, t, _ = words.shape
    return unpack_weight(words.reshape(g, 128, t, 2, 2).transpose(0, 3, 1, 2, 4).reshape(2 * g, 128, 2 * t), scales, "e2m1")


def silu(f):
    return f / (1.0 + np.exp(-np.maximum(f, -700.0)))


K, R, N, T, J = 1024, 512, 256, 2048, 1024


def setup_inputs():
    n = np.random.standard_normal
    s = mx_kscale(K)[:, None]
    u = mx_kscale(R)[:, None]
    p_tab = pack_table4(n((K, T)) * s)
    return {
        "tab_words": p_tab[0],
        "tab_scales": p_tab[1],
        "w0": (n((K, R)) / np.sqrt(3 * K) / s).astype(np.float32),
        "w1": (n((K, R)) / np.sqrt(3 * K) / s).astype(np.float32),
        "w2": (n((K, R)) / np.sqrt(3 * K) / s).astype(np.float32),
        "sm": (np.random.uniform(0.5, 2.0, R) * u[:, 0]).astype(np.float32),
        "wd": (n((R, N)) / np.sqrt(R) / u).astype(np.float32),
        "b": (0.3 * n(N)).astype(np.float32),
        "offs": striped(np.concatenate([np.random.permutation(T)[:J] for _ in range(3)])),
    }


def reference(tab_words, tab_scales, w0, w1, w2, sm, wd, b, offs):
    idx = unstriped(offs).reshape(3, J)
    tab_ = unpack_table4(tab_words, tab_scales)[:, idx]
    w0_ = mxq(f64(w0), 0, "e4m3")
    w1_ = mxq(f64(w1), 0, "e4m3")
    w2_ = mxq(f64(w2), 0, "e4m3")
    a = w0_.T @ tab_[:, 0] + w1_.T @ tab_[:, 1] + w2_.T @ tab_[:, 2]
    h = f64(sm)[:, None] * silu(a)
    h_ = mxq(h, 0, "e4m3")
    wd_ = mxq(f64(wd), 0, "e4m3")
    y = wd_.T @ h_
    return y + f64(b)[:, None]

@@ -1,0 +1,192 @@
+from contextlib import ExitStack
+
+import concourse.mybir as mybir
+
+K, R, N, T, J = 1024, 512, 256, 2048, 1024
+FLOPS = 2 * (3 * K * R * J + R * N * J)
+
+F32 = mybir.dt.float32
+BF16 = mybir.dt.bfloat16
+I32 = mybir.dt.int32
+U32 = mybir.dt.uint32
+U16 = mybir.dt.uint16
+U8 = mybir.dt.uint8
+FP8X4 = mybir.dt.float8_e4m3fn_x4
+FP4X4 = mybir.dt.float4_e2m1fn_x4
+ACT = mybir.ActivationFunctionType
+ALU = mybir.AluOpType
+
+P = 128
+PACK = 4
+PASS = P * PACK
+LISTS = 3
+PASSES = K // PASS
+JB = 128
+BANKS = J // JB
+HALF = J // 2
+
+
+def tile_list_rvq_fff_silu_bias_kernel(tc, tab_words, tab_scales, w0, w1, w2, sm, wd, b, offs, out):
+    nc = tc.nc
+    weights = (w0, w1, w2)
+
+    with ExitStack() as ctx:
+        keep = ctx.enter_context(tc.tile_pool(name="keep", bufs=1))
+        ring = ctx.enter_context(tc.tile_pool(name="ring", bufs=3))
+        psum = ctx.enter_context(tc.psum_pool(name="psum", bufs=1))
+
+        offsets = keep.tile([P, LISTS * J // 16], U16, name="offsets")
+        table_scales = keep.tile([P, T], U8, name="table_scales", align_bytes=64)
+        nc.gpsimd.memset(table_scales[:].bitcast(I32), 0)
+        second_scales = [keep.tile([P, J], U8, name=f"second_scales{g}", align_bytes=64) for g in range(LISTS)]
+        for plane in second_scales:
+            nc.gpsimd.memset(plane[:].bitcast(I32), 0)
+
+        nc.sync.dma_start(offsets[:], offs)
+        smooth = keep.tile([P, PACK], F32, name="smooth")
+        nc.sync.dma_start(smooth[:], sm.rearrange("(p t) -> p t", t=PACK))
+        bias = keep.tile([P, N // P], F32, name="bias")
+        with nc.allow_non_contiguous_dma(reason="one bias value a partition"):
+            nc.sync.dma_start(bias[:], b.rearrange("(c p) -> p c", p=P))
+        warm = keep.tile([P, 1], F32, name="warm")
+        nc.scalar.activation(warm[:], smooth[:, 0:1], ACT.Silu)
+        scale_rows = tab_scales.bitcast(I32).rearrange("a (q r) n -> r q a n", r=4)
+        for r in range(4):
+            nc.sync.dma_start(table_scales[r:P:16, :].bitcast(I32), scale_rows[r])
+        table_words = keep.tile([P, T], I32, name="table_words", align_bytes=64)
+        nc.sync.dma_start(table_words[:], tab_words[0].rearrange("p t b -> p (t b)").bitcast(I32))
+
+        raw = {}
+
+        def load_weight(g, d):
+            rows = weights[g][d * PASS:(d + 1) * PASS, :].rearrange("(p i) r -> p i r", i=PACK)
+            parts = 2 if (g, d) == (0, 0) else 1
+            width = R // parts
+            raw[g, d] = []
+            for s in range(parts):
+                tag = f"raw{(PASSES * g + d) % 3}" if s == parts - 1 else "raw_head"
+                piece = keep.tile([P, PACK, width], F32, name=f"raw{g}{d}{s}", tag=tag)
+                nc.sync.dma_start(piece[:], rows[:, :, s * width:(s + 1) * width])
+                raw[g, d].append(piece)
+
+        load_weight(0, 0)
+        load_weight(0, 1)
+        load_weight(1, 0)
+
+        codes, scales = {}, {}
+
+        def round_and_quantise(g, d, tag):
+            rounded = keep.tile([P, PACK * R], BF16, name=f"rounded{g}{d}", tag=tag, align_bytes=64)
+            view = rounded[:].rearrange("p (t m i) -> p m i t", t=PACK, i=PACK)
+            width = P // len(raw[g, d])
+            for s, piece in enumerate(raw[g, d]):
+                nc.scalar.copy(view[:, s * width:(s + 1) * width], piece[:].rearrange("p i (m t) -> p m i t", t=PACK))
+            codes[g, d] = keep.tile([P, R], U32, name=f"codes{g}{d}", align_bytes=64)
+            scales[g, d] = keep.tile([P, R], U8, name=f"scales{g}{d}", align_bytes=64)
+            nc.vector.quantize_mx(codes[g, d][:].bitcast(FP8X4), scales[g, d][:], rounded[:])
+
+        first_scales = {}
+
+        def gather_scales(g, tag, queue):
+            first_scales[g] = keep.tile([P, J], U8, name=f"first_scales{g}", tag=tag, align_bytes=64)
+            listed = offsets[:, g * J // 16:(g + 1) * J // 16]
+            nc.vector.tensor_copy(first_scales[g][:], table_scales[:].indirect(listed))
+            for r in range(4):
+                queue.dma_start(second_scales[g][r:P:32, :].bitcast(I32), first_scales[g][16 + r:P:32, :].bitcast(I32))
+
+        parted = {}
+
+        def gather_words(g, j0, width, tag):
+            picked = keep.tile([P, width], U32, name=f"picked{g}_{j0}", tag=tag, align_bytes=64)
+            listed = offsets[:, (g * J + j0) // 16:(g * J + j0 + width) // 16]
+            nc.vector.tensor_copy(picked[:], table_words[:].bitcast(U32).indirect(listed))
+            halves = keep.tile([P, PASSES, 2 * width], U8, name=f"parted{g}_{j0}", align_bytes=64)
+            nc.vector.tensor_copy(halves[:].bitcast(U16), picked[:].bitcast(U16).rearrange("p (j d) -> p d j", d=PASSES))
+            for j in range(j0, j0 + width, JB):
+                parted[g, j // JB] = (halves, j - j0)
+
+        banks = [psum.tile([P, PACK, JB], F32, name=f"bank{c}", tag=f"bank{c}") for c in range(BANKS)]
+
+        def first_layer(g, d, c):
+            halves, j0 = parted[g, c]
+            plane = (first_scales, second_scales)[d][g]
+            for t in range(PACK):
+                nc.tensor.matmul_mx(
+                    banks[c][:, t, :],
+                    lhsT=codes[g, d][:, t * P:(t + 1) * P].bitcast(FP8X4),
+                    lhsT_scale=scales[g, d][:, t * P:(t + 1) * P],
+                    rhs=halves[:, d, 2 * j0:2 * (j0 + JB)].bitcast(FP4X4),
+                    rhs_scale=plane[:, c * JB:(c + 1) * JB],
+                    start=(g, d, t) == (0, 0, 0),
+                    stop=(g, d, t) == (LISTS - 1, PASSES - 1, PACK - 1),
+                )
+
+        gather_scales(0, "s0", nc.sync)
+        gather_words(0, 0, J, "p0")
+        round_and_quantise(0, 0, "a")
+        load_weight(1, 1)
+        for c in range(BANKS):
+            first_layer(0, 0, c)
+        gather_scales(1, "a", nc.sync)
+        round_and_quantise(0, 1, "b")
+        load_weight(2, 0)
+        for c in range(BANKS):
+            first_layer(0, 1, c)
+        gather_words(1, 0, J, "b")
+        round_and_quantise(1, 0, "c")
+        load_weight(2, 1)
+        for c in range(BANKS):
+            first_layer(1, 0, c)
+        gather_scales(2, "c", nc.sync)
+        round_and_quantise(1, 1, "d")
+        raw_down = keep.tile([P, PACK, N], F32, name="raw_down", tag="raw0")
+        nc.sync.dma_start(raw_down[:], wd.rearrange("(p i) n -> p i n", i=PACK))
+        for c in range(BANKS):
+            first_layer(1, 1, c)
+        gather_words(2, 0, HALF, "d")
+        round_and_quantise(2, 0, "e")
+        for c in range(BANKS // 2):
+            first_layer(2, 0, c)
+        round_and_quantise(2, 1, "f")
+        for c in range(BANKS // 2):
+            first_layer(2, 1, c)
+        gather_words(2, HALF, HALF, "f")
+        for c in range(BANKS // 2, BANKS):
+            first_layer(2, 0, c)
+            first_layer(2, 1, c)
+
+        rounded_down = keep.tile([P, PACK * N], BF16, name="rounded_down", align_bytes=64)
+        nc.scalar.copy(
+            rounded_down[:].rearrange("p (m u i) -> p m i u", u=4, i=PACK),
+            raw_down[:].rearrange("p i (m u) -> p m i u", u=4),
+        )
+        down_codes = keep.tile([P, N], U32, name="down_codes", align_bytes=64)
+        down_scales = keep.tile([P, N], U8, name="down_scales", align_bytes=64)
+        nc.vector.quantize_mx(down_codes[:].bitcast(FP8X4), down_scales[:], rounded_down[:])
+
+        out_rows = out.rearrange("(c p) j -> p c j", p=P)
+        pair = 2
+        for c0 in range(0, BANKS, pair):
+            hidden = ring.tile([P, pair, JB, PACK], BF16, name="hidden", align_bytes=64)
+            for c in range(c0, c0 + pair):
+                active = ring.tile([P, JB, PACK], F32, name="active")
+                nc.scalar.activation(active[:], banks[c][:].rearrange("p t j -> p j t"), ACT.Silu)
+                nc.vector.tensor_tensor(hidden[:, c - c0], active[:], smooth[:].unsqueeze(1).to_broadcast([P, JB, PACK]), ALU.mult)
+            hidden_codes = ring.tile([P, pair * JB], U32, name="hidden_codes", align_bytes=64)
+            hidden_scales = ring.tile([P, pair * JB], U8, name="hidden_scales", align_bytes=64)
+            nc.vector.quantize_mx(hidden_codes[:].bitcast(FP8X4), hidden_scales[:], hidden[:].rearrange("p c j t -> p (c j t)"))
+            y = psum.tile([P, N // P, pair * JB], F32, name=f"y{c0}", tag=f"bank{c0}")
+            result = ring.tile([P, N // P, pair * JB], F32, name="result")
+            for c in range(N // P):
+                nc.tensor.matmul_mx(
+                    y[:, c, :],
+                    lhsT=down_codes[:, c * P:(c + 1) * P].bitcast(FP8X4),
+                    lhsT_scale=down_scales[:, c * P:(c + 1) * P],
+                    rhs=hidden_codes[:].bitcast(FP8X4),
+                    rhs_scale=hidden_scales[:],
+                    start=True,
+                    stop=True,
+                )
+            for c in range(N // P):
+                nc.scalar.activation(result[:, c, :], y[:, c, :], ACT.Identity, bias=bias[:, c:c + 1])
+            nc.sync.dma_start(out_rows[:, :, c0 * JB:(c0 + pair) * JB], result[:])

@@ -43,11 +43,10 @@ def tile_list_rvq_fff_silu_bias_kernel(tc, tab_words, tab_scales, w0, w1, w2, sm
             nc.gpsimd.memset(plane[:].bitcast(I32), 0)
 
         nc.sync.dma_start(offsets[:], offs)
-        smooth = keep.tile([P, PACK], F32, name="smooth")
-        nc.sync.dma_start(smooth[:], sm.rearrange("(p t) -> p t", t=PACK))
-        bias = keep.tile([P, N // P], F32, name="bias")
-        with nc.allow_non_contiguous_dma(reason="one bias value a partition"):
-            nc.sync.dma_start(bias[:], b.rearrange("(c p) -> p c", p=P))
+        smooth = keep.tile([P, 7], F32, name="smooth")
+        smooth_rows = sm.rearrange("(c e) -> c e", e=8)
+        for u in range(2):
+            nc.sync.dma_start(smooth[u:P:2, :], smooth_rows[:, u:u + 7])
         warm = keep.tile([P, 1], F32, name="warm")
         nc.scalar.activation(warm[:], smooth[:, 0:1], ACT.Silu)
         scale_rows = tab_scales.bitcast(I32).rearrange("a (q r) n -> r q a n", r=4)
@@ -72,15 +71,18 @@ def tile_list_rvq_fff_silu_bias_kernel(tc, tab_words, tab_scales, w0, w1, w2, sm
         load_weight(0, 0)
         load_weight(0, 1)
         load_weight(1, 0)
+        bias = keep.tile([P, N // P], F32, name="bias")
+        with nc.allow_non_contiguous_dma(reason="one bias value a partition"):
+            nc.sync.dma_start(bias[:], b.rearrange("(c p) -> p c", p=P))
 
         codes, scales = {}, {}
 
         def round_and_quantise(g, d, tag):
             rounded = keep.tile([P, PACK * R], BF16, name=f"rounded{g}{d}", tag=tag, align_bytes=64)
-            view = rounded[:].rearrange("p (t m i) -> p m i t", t=PACK, i=PACK)
-            width = P // len(raw[g, d])
+            view = rounded[:].rearrange("p (t c u i) -> p c t i u", t=PACK, u=2, i=PACK)
+            width = P // 2 // len(raw[g, d])
             for s, piece in enumerate(raw[g, d]):
-                nc.scalar.copy(view[:, s * width:(s + 1) * width], piece[:].rearrange("p i (m t) -> p m i t", t=PACK))
+                nc.scalar.copy(view[:, s * width:(s + 1) * width], piece[:].rearrange("p i (c t u) -> p c t i u", t=PACK, u=2))
             codes[g, d] = keep.tile([P, R], U32, name=f"codes{g}{d}", align_bytes=64)
             scales[g, d] = keep.tile([P, R], U8, name=f"scales{g}{d}", align_bytes=64)
             nc.vector.quantize_mx(codes[g, d][:].bitcast(FP8X4), scales[g, d][:], rounded[:])
@@ -100,8 +102,15 @@ def tile_list_rvq_fff_silu_bias_kernel(tc, tab_words, tab_scales, w0, w1, w2, sm
             picked = keep.tile([P, width], U32, name=f"picked{g}_{j0}", tag=tag, align_bytes=64)
             listed = offsets[:, (g * J + j0) // 16:(g * J + j0 + width) // 16]
             nc.vector.tensor_copy(picked[:], table_words[:].bitcast(U32).indirect(listed))
-            halves = keep.tile([P, PASSES, 2 * width], U8, name=f"parted{g}_{j0}", align_bytes=64)
-            nc.vector.tensor_copy(halves[:].bitcast(U16), picked[:].bitcast(U16).rearrange("p (j d) -> p d j", d=PASSES))
+            return picked
+
+        def part_words(g, j0, picked, tag):
+            width = picked.shape[1]
+            halves = keep.tile([P, PASSES, 2 * width], U8, name=f"parted{g}_{j0}", tag=tag, align_bytes=64)
+            nc.vector.tensor_copy(
+                halves[:].bitcast(U16).rearrange("p d (j e) -> p j d e", e=8),
+                picked[:].bitcast(U16).rearrange("p (j e d) -> p j d e", e=8, d=PASSES),
+            )
             for j in range(j0, j0 + width, JB):
                 parted[g, j // JB] = (halves, j - j0)
 
@@ -122,7 +131,7 @@ def tile_list_rvq_fff_silu_bias_kernel(tc, tab_words, tab_scales, w0, w1, w2, sm
                 )
 
         gather_scales(0, "s0", nc.sync)
-        gather_words(0, 0, J, "p0")
+        part_words(0, 0, gather_words(0, 0, J, "p0"), "q0")
         round_and_quantise(0, 0, "a")
         load_weight(1, 1)
         for c in range(BANKS):
@@ -132,51 +141,54 @@ def tile_list_rvq_fff_silu_bias_kernel(tc, tab_words, tab_scales, w0, w1, w2, sm
         load_weight(2, 0)
         for c in range(BANKS):
             first_layer(0, 1, c)
-        gather_words(1, 0, J, "b")
+        picked = gather_words(1, 0, J, "b")
         round_and_quantise(1, 0, "c")
         load_weight(2, 1)
+        part_words(1, 0, picked, "c")
         for c in range(BANKS):
             first_layer(1, 0, c)
-        gather_scales(2, "c", nc.sync)
+        gather_scales(2, "b", nc.sync)
         round_and_quantise(1, 1, "d")
         raw_down = keep.tile([P, PACK, N], F32, name="raw_down", tag="raw0")
-        nc.sync.dma_start(raw_down[:], wd.rearrange("(p i) n -> p i n", i=PACK))
+        down_rows = wd.rearrange("(c t u) n -> u c t n", t=PACK, u=2)
+        for u in range(2):
+            nc.sync.dma_start(raw_down[u:P:2], down_rows[u])
         for c in range(BANKS):
             first_layer(1, 1, c)
-        gather_words(2, 0, HALF, "d")
+        picked = gather_words(2, 0, HALF, "d")
         round_and_quantise(2, 0, "e")
+        part_words(2, 0, picked, "e")
         for c in range(BANKS // 2):
             first_layer(2, 0, c)
         round_and_quantise(2, 1, "f")
         for c in range(BANKS // 2):
             first_layer(2, 1, c)
-        gather_words(2, HALF, HALF, "f")
+        part_words(2, HALF, gather_words(2, HALF, HALF, "f"), "q2")
         for c in range(BANKS // 2, BANKS):
             first_layer(2, 0, c)
             first_layer(2, 1, c)
 
         rounded_down = keep.tile([P, PACK * N], BF16, name="rounded_down", align_bytes=64)
         nc.scalar.copy(
-            rounded_down[:].rearrange("p (m u i) -> p m i u", u=4, i=PACK),
-            raw_down[:].rearrange("p i (m u) -> p m i u", u=4),
+            rounded_down[:].rearrange("p (m u i) -> p m i u", u=2, i=PACK),
+            raw_down[:].rearrange("p i (m u) -> p m i u", u=2),
         )
         down_codes = keep.tile([P, N], U32, name="down_codes", align_bytes=64)
         down_scales = keep.tile([P, N], U8, name="down_scales", align_bytes=64)
         nc.vector.quantize_mx(down_codes[:].bitcast(FP8X4), down_scales[:], rounded_down[:])
 
         out_rows = out.rearrange("(c p) j -> p c j", p=P)
-        pair = 2
-        for c0 in range(0, BANKS, pair):
+        for c0, pair in ((0, 2), (2, 2), (4, 2), (6, 1), (7, 1)):
             hidden = ring.tile([P, pair, JB, PACK], BF16, name="hidden", align_bytes=64)
             for c in range(c0, c0 + pair):
-                active = ring.tile([P, JB, PACK], F32, name="active")
+                active = ring.tile([P, JB, PACK], F32, name="active", bufs=BANKS)
                 nc.scalar.activation(active[:], banks[c][:].rearrange("p t j -> p j t"), ACT.Silu)
-                nc.vector.tensor_tensor(hidden[:, c - c0], active[:], smooth[:].unsqueeze(1).to_broadcast([P, JB, PACK]), ALU.mult)
+                nc.vector.tensor_tensor(hidden[:, c - c0], active[:], smooth[:, 0:7:2].unsqueeze(1).to_broadcast([P, JB, PACK]), ALU.mult)
             hidden_codes = ring.tile([P, pair * JB], U32, name="hidden_codes", align_bytes=64)
             hidden_scales = ring.tile([P, pair * JB], U8, name="hidden_scales", align_bytes=64)
             nc.vector.quantize_mx(hidden_codes[:].bitcast(FP8X4), hidden_scales[:], hidden[:].rearrange("p c j t -> p (c j t)"))
             y = psum.tile([P, N // P, pair * JB], F32, name=f"y{c0}", tag=f"bank{c0}")
-            result = ring.tile([P, N // P, pair * JB], F32, name="result")
+            result = ring.tile([P, N // P, pair * JB], F32, name="result", bufs=5)
             for c in range(N // P):
                 nc.tensor.matmul_mx(
                     y[:, c, :],

@@ -24,6 +24,7 @@ PASSES = K // PASS
 JB = 128
 BANKS = J // JB
 HALF = J // 2
+RUNS = ((0, 3 * HALF), (3 * HALF, 5 * HALF), (5 * HALF, 6 * HALF))
 
 
 def tile_list_rvq_fff_silu_bias_kernel(tc, tab_words, tab_scales, w0, w1, w2, sm, wd, b, offs, out):
@@ -37,8 +38,8 @@ def tile_list_rvq_fff_silu_bias_kernel(tc, tab_words, tab_scales, w0, w1, w2, sm
 
         offsets = keep.tile([P, LISTS * J // 16], U16, name="offsets")
         table_scales = keep.tile([P, T], U8, name="table_scales", align_bytes=64)
-        nc.gpsimd.memset(table_scales[:].bitcast(I32), 0)
-        second_scales = [keep.tile([P, J], U8, name=f"second_scales{g}", align_bytes=64) for g in range(LISTS)]
+        nc.vector.memset(table_scales[:].bitcast(I32), 0)
+        second_scales = [keep.tile([P, m1 - m0], U8, name=f"second_scales{m0}", align_bytes=64) for m0, m1 in RUNS]
         for plane in second_scales:
             nc.gpsimd.memset(plane[:].bitcast(I32), 0)
 
@@ -49,6 +50,8 @@ def tile_list_rvq_fff_silu_bias_kernel(tc, tab_words, tab_scales, w0, w1, w2, sm
             nc.sync.dma_start(smooth[u:P:2, :], smooth_rows[:, u:u + 7])
         warm = keep.tile([P, 1], F32, name="warm")
         nc.scalar.activation(warm[:], smooth[:, 0:1], ACT.Silu)
+        smooth_wide = keep.tile([P, JB, PACK], F32, name="smooth_wide")
+        nc.scalar.copy(smooth_wide[:], smooth[:, 0:7:2].unsqueeze(1).to_broadcast([P, JB, PACK]))
         scale_rows = tab_scales.bitcast(I32).rearrange("a (q r) n -> r q a n", r=4)
         for r in range(4):
             nc.sync.dma_start(table_scales[r:P:16, :].bitcast(I32), scale_rows[r])
@@ -57,23 +60,19 @@ def tile_list_rvq_fff_silu_bias_kernel(tc, tab_words, tab_scales, w0, w1, w2, sm
 
         raw = {}
 
-        def load_weight(g, d):
+        def load_weight(g, d, tags):
             rows = weights[g][d * PASS:(d + 1) * PASS, :].rearrange("(p i) r -> p i r", i=PACK)
-            parts = 2 if (g, d) == (0, 0) else 1
+            parts = len(tags)
             width = R // parts
             raw[g, d] = []
-            for s in range(parts):
-                tag = f"raw{(PASSES * g + d) % 3}" if s == parts - 1 else "raw_head"
-                piece = keep.tile([P, PACK, width], F32, name=f"raw{g}{d}{s}", tag=tag)
+            for s, tag in enumerate(tags):
+                piece = keep.tile([P, PACK, width], F32, name=f"raw{g}{d}{s}", tag=tag, align_bytes=64)
                 nc.sync.dma_start(piece[:], rows[:, :, s * width:(s + 1) * width])
                 raw[g, d].append(piece)
 
-        load_weight(0, 0)
-        load_weight(0, 1)
-        load_weight(1, 0)
-        bias = keep.tile([P, N // P], F32, name="bias")
-        with nc.allow_non_contiguous_dma(reason="one bias value a partition"):
-            nc.sync.dma_start(bias[:], b.rearrange("(c p) -> p c", p=P))
+        load_weight(0, 0, ("raw0", "raw1"))
+        load_weight(0, 1, ("raw2",))
+        load_weight(1, 0, ("raw3",))
 
         codes, scales = {}, {}
 
@@ -89,12 +88,13 @@ def tile_list_rvq_fff_silu_bias_kernel(tc, tab_words, tab_scales, w0, w1, w2, sm
 
         first_scales = {}
 
-        def gather_scales(g, tag, queue):
-            first_scales[g] = keep.tile([P, J], U8, name=f"first_scales{g}", tag=tag, align_bytes=64)
-            listed = offsets[:, g * J // 16:(g + 1) * J // 16]
-            nc.vector.tensor_copy(first_scales[g][:], table_scales[:].indirect(listed))
+        def gather_scales(s, tag):
+            m0, m1 = RUNS[s]
+            first_scales[s] = keep.tile([P, m1 - m0], U8, name=f"first_scales{s}", tag=tag, align_bytes=64)
+            listed = offsets[:, m0 // 16:m1 // 16]
+            nc.vector.tensor_copy(first_scales[s][:], table_scales[:].indirect(listed))
             for r in range(4):
-                queue.dma_start(second_scales[g][r:P:32, :].bitcast(I32), first_scales[g][16 + r:P:32, :].bitcast(I32))
+                nc.sync.dma_start(second_scales[s][r:P:32, :].bitcast(I32), first_scales[s][16 + r:P:32, :].bitcast(I32))
 
         parted = {}
 
@@ -108,8 +108,8 @@ def tile_list_rvq_fff_silu_bias_kernel(tc, tab_words, tab_scales, w0, w1, w2, sm
             width = picked.shape[1]
             halves = keep.tile([P, PASSES, 2 * width], U8, name=f"parted{g}_{j0}", tag=tag, align_bytes=64)
             nc.vector.tensor_copy(
-                halves[:].bitcast(U16).rearrange("p d (j e) -> p j d e", e=8),
-                picked[:].bitcast(U16).rearrange("p (j e d) -> p j d e", e=8, d=PASSES),
+                halves[:].bitcast(U16).rearrange("p d (h j) -> p h d j", h=2),
+                picked[:].bitcast(U16).rearrange("p (h j d) -> p h d j", h=2, d=PASSES),
             )
             for j in range(j0, j0 + width, JB):
                 parted[g, j // JB] = (halves, j - j0)
@@ -118,72 +118,80 @@ def tile_list_rvq_fff_silu_bias_kernel(tc, tab_words, tab_scales, w0, w1, w2, sm
 
         def first_layer(g, d, c):
             halves, j0 = parted[g, c]
-            plane = (first_scales, second_scales)[d][g]
+            entry = g * J + c * JB
+            s = max(n for n, run in enumerate(RUNS) if run[0] <= entry)
+            m0 = entry - RUNS[s][0]
+            plane = (first_scales, second_scales)[d][s]
             for t in range(PACK):
                 nc.tensor.matmul_mx(
                     banks[c][:, t, :],
                     lhsT=codes[g, d][:, t * P:(t + 1) * P].bitcast(FP8X4),
                     lhsT_scale=scales[g, d][:, t * P:(t + 1) * P],
                     rhs=halves[:, d, 2 * j0:2 * (j0 + JB)].bitcast(FP4X4),
-                    rhs_scale=plane[:, c * JB:(c + 1) * JB],
+                    rhs_scale=plane[:, m0:m0 + JB],
                     start=(g, d, t) == (0, 0, 0),
                     stop=(g, d, t) == (LISTS - 1, PASSES - 1, PACK - 1),
                 )
 
-        gather_scales(0, "s0", nc.sync)
+        gather_scales(0, "s0")
         part_words(0, 0, gather_words(0, 0, J, "p0"), "q0")
         round_and_quantise(0, 0, "a")
-        load_weight(1, 1)
+        load_weight(1, 1, ("raw0",))
+        load_weight(2, 0, ("raw1",))
         for c in range(BANKS):
             first_layer(0, 0, c)
-        gather_scales(1, "a", nc.sync)
+        picked = gather_words(1, 0, J, "a")
         round_and_quantise(0, 1, "b")
-        load_weight(2, 0)
+        load_weight(2, 1, ("raw2",))
         for c in range(BANKS):
             first_layer(0, 1, c)
-        picked = gather_words(1, 0, J, "b")
+        part_words(1, 0, picked, "b")
         round_and_quantise(1, 0, "c")
-        load_weight(2, 1)
-        part_words(1, 0, picked, "c")
-        for c in range(BANKS):
-            first_layer(1, 0, c)
-        gather_scales(2, "b", nc.sync)
-        round_and_quantise(1, 1, "d")
-        raw_down = keep.tile([P, PACK, N], F32, name="raw_down", tag="raw0")
+        raw_down = keep.tile([P, PACK, N], F32, name="raw_down", tag="raw3", align_bytes=64)
         down_rows = wd.rearrange("(c t u) n -> u c t n", t=PACK, u=2)
         for u in range(2):
             nc.sync.dma_start(raw_down[u:P:2], down_rows[u])
+        for c in range(BANKS // 2):
+            first_layer(1, 0, c)
+        gather_scales(1, "c")
+        for c in range(BANKS // 2, BANKS):
+            first_layer(1, 0, c)
+        round_and_quantise(1, 1, "d")
+        bias = keep.tile([P, N // P], F32, name="bias", tag="raw0", align_bytes=64)
+        nc.sync.dma_start(bias[:], b.rearrange("(p c) -> p c", p=P))
         for c in range(BANKS):
             first_layer(1, 1, c)
         picked = gather_words(2, 0, HALF, "d")
         round_and_quantise(2, 0, "e")
         part_words(2, 0, picked, "e")
+        gather_scales(2, "d")
         for c in range(BANKS // 2):
             first_layer(2, 0, c)
         round_and_quantise(2, 1, "f")
         for c in range(BANKS // 2):
             first_layer(2, 1, c)
-        part_words(2, HALF, gather_words(2, HALF, HALF, "f"), "q2")
-        for c in range(BANKS // 2, BANKS):
-            first_layer(2, 0, c)
-            first_layer(2, 1, c)
-
-        rounded_down = keep.tile([P, PACK * N], BF16, name="rounded_down", align_bytes=64)
+        picked = gather_words(2, HALF, HALF, "f")
+        rounded_down = keep.tile([P, PACK * N], BF16, name="rounded_down", tag="raw2", align_bytes=64)
         nc.scalar.copy(
-            rounded_down[:].rearrange("p (m u i) -> p m i u", u=2, i=PACK),
-            raw_down[:].rearrange("p i (m u) -> p m i u", u=2),
+            rounded_down[:].rearrange("p (c m u i) -> p m c i u", c=2, u=2, i=PACK),
+            raw_down[:].rearrange("p i (m u c) -> p m c i u", u=2, c=2),
         )
         down_codes = keep.tile([P, N], U32, name="down_codes", align_bytes=64)
         down_scales = keep.tile([P, N], U8, name="down_scales", align_bytes=64)
         nc.vector.quantize_mx(down_codes[:].bitcast(FP8X4), down_scales[:], rounded_down[:])
+        part_words(2, HALF, picked, "raw2")
+        for c in range(BANKS // 2, BANKS):
+            first_layer(2, 0, c)
+            first_layer(2, 1, c)
 
-        out_rows = out.rearrange("(c p) j -> p c j", p=P)
+
+        out_rows = out.rearrange("(p c) j -> p c j", p=P)
         for c0, pair in ((0, 2), (2, 2), (4, 2), (6, 1), (7, 1)):
             hidden = ring.tile([P, pair, JB, PACK], BF16, name="hidden", align_bytes=64)
             for c in range(c0, c0 + pair):
                 active = ring.tile([P, JB, PACK], F32, name="active", bufs=BANKS)
                 nc.scalar.activation(active[:], banks[c][:].rearrange("p t j -> p j t"), ACT.Silu)
-                nc.vector.tensor_tensor(hidden[:, c - c0], active[:], smooth[:, 0:7:2].unsqueeze(1).to_broadcast([P, JB, PACK]), ALU.mult)
+                nc.vector.tensor_tensor(hidden[:, c - c0], active[:], smooth_wide[:], ALU.mult)
             hidden_codes = ring.tile([P, pair * JB], U32, name="hidden_codes", align_bytes=64)
             hidden_scales = ring.tile([P, pair * JB], U8, name="hidden_scales", align_bytes=64)
             nc.vector.quantize_mx(hidden_codes[:].bitcast(FP8X4), hidden_scales[:], hidden[:].rearrange("p c j t -> p (c j t)"))

@@ -24,6 +24,7 @@ PASSES = K // PASS
 JB = 128
 BANKS = J // JB
 HALF = J // 2
+GROUPS = ((0, 2), (2, 2), (4, 2), (6, 1), (7, 1))
 RUNS = ((0, 3 * HALF), (3 * HALF, 5 * HALF), (5 * HALF, 6 * HALF))
 
 
@@ -33,7 +34,6 @@ def tile_list_rvq_fff_silu_bias_kernel(tc, tab_words, tab_scales, w0, w1, w2, sm
 
     with ExitStack() as ctx:
         keep = ctx.enter_context(tc.tile_pool(name="keep", bufs=1))
-        ring = ctx.enter_context(tc.tile_pool(name="ring", bufs=3))
         psum = ctx.enter_context(tc.psum_pool(name="psum", bufs=1))
 
         offsets = keep.tile([P, LISTS * J // 16], U16, name="offsets")
@@ -48,8 +48,6 @@ def tile_list_rvq_fff_silu_bias_kernel(tc, tab_words, tab_scales, w0, w1, w2, sm
         smooth_rows = sm.rearrange("(c e) -> c e", e=8)
         for u in range(2):
             nc.sync.dma_start(smooth[u:P:2, :], smooth_rows[:, u:u + 7])
-        warm = keep.tile([P, 1], F32, name="warm")
-        nc.scalar.activation(warm[:], smooth[:, 0:1], ACT.Silu)
         smooth_wide = keep.tile([P, JB, PACK], F32, name="smooth_wide")
         nc.scalar.copy(smooth_wide[:], smooth[:, 0:7:2].unsqueeze(1).to_broadcast([P, JB, PACK]))
         scale_rows = tab_scales.bitcast(I32).rearrange("a (q r) n -> r q a n", r=4)
@@ -70,14 +68,14 @@ def tile_list_rvq_fff_silu_bias_kernel(tc, tab_words, tab_scales, w0, w1, w2, sm
                 nc.sync.dma_start(piece[:], rows[:, :, s * width:(s + 1) * width])
                 raw[g, d].append(piece)
 
-        load_weight(0, 0, ("raw0", "raw1"))
-        load_weight(0, 1, ("raw2",))
-        load_weight(1, 0, ("raw3",))
+        load_weight(0, 0, ("raw00a", "raw00b"))
+        load_weight(0, 1, ("raw01a", "raw01b"))
+        load_weight(1, 0, ("raw10",))
 
         codes, scales = {}, {}
 
-        def round_and_quantise(g, d, tag):
-            rounded = keep.tile([P, PACK * R], BF16, name=f"rounded{g}{d}", tag=tag, align_bytes=64)
+        def round_and_quantise(g, d):
+            rounded = keep.tile([P, PACK * R], BF16, name=f"rounded{g}{d}", tag=f"rounded{g}{d}", align_bytes=64)
             view = rounded[:].rearrange("p (t c u i) -> p c t i u", t=PACK, u=2, i=PACK)
             width = P // 2 // len(raw[g, d])
             for s, piece in enumerate(raw[g, d]):
@@ -133,45 +131,45 @@ def tile_list_rvq_fff_silu_bias_kernel(tc, tab_words, tab_scales, w0, w1, w2, sm
                     stop=(g, d, t) == (LISTS - 1, PASSES - 1, PACK - 1),
                 )
 
-        gather_scales(0, "s0")
-        part_words(0, 0, gather_words(0, 0, J, "p0"), "q0")
-        round_and_quantise(0, 0, "a")
-        load_weight(1, 1, ("raw0",))
-        load_weight(2, 0, ("raw1",))
+        gather_scales(0, "scales0")
+        part_words(0, 0, gather_words(0, 0, J, "picked0"), "parted0")
+        round_and_quantise(0, 0)
+        load_weight(1, 1, ("raw00a",))
+        load_weight(2, 0, ("rounded00",))
         for c in range(BANKS):
             first_layer(0, 0, c)
-        picked = gather_words(1, 0, J, "a")
-        round_and_quantise(0, 1, "b")
-        load_weight(2, 1, ("raw2",))
+        picked = gather_words(1, 0, J, "raw00b")
+        round_and_quantise(0, 1)
+        load_weight(2, 1, ("raw01a",))
         for c in range(BANKS):
             first_layer(0, 1, c)
-        part_words(1, 0, picked, "b")
-        round_and_quantise(1, 0, "c")
-        raw_down = keep.tile([P, PACK, N], F32, name="raw_down", tag="raw3", align_bytes=64)
+        part_words(1, 0, picked, "raw01b")
+        round_and_quantise(1, 0)
+        raw_down = keep.tile([P, PACK, N], F32, name="raw_down", tag="raw00b", align_bytes=64)
         down_rows = wd.rearrange("(c t u) n -> u c t n", t=PACK, u=2)
         for u in range(2):
             nc.sync.dma_start(raw_down[u:P:2], down_rows[u])
         for c in range(BANKS // 2):
             first_layer(1, 0, c)
-        gather_scales(1, "c")
+        gather_scales(1, "raw10")
         for c in range(BANKS // 2, BANKS):
             first_layer(1, 0, c)
-        round_and_quantise(1, 1, "d")
-        bias = keep.tile([P, N // P], F32, name="bias", tag="raw0", align_bytes=64)
+        round_and_quantise(1, 1)
+        bias = keep.tile([P, N // P], F32, name="bias", tag="rounded10", align_bytes=64)
         nc.sync.dma_start(bias[:], b.rearrange("(p c) -> p c", p=P))
         for c in range(BANKS):
             first_layer(1, 1, c)
-        picked = gather_words(2, 0, HALF, "d")
-        round_and_quantise(2, 0, "e")
-        part_words(2, 0, picked, "e")
-        gather_scales(2, "d")
+        picked = gather_words(2, 0, HALF, "raw00a")
+        round_and_quantise(2, 0)
+        part_words(2, 0, picked, "rounded00")
+        gather_scales(2, "rounded20")
         for c in range(BANKS // 2):
             first_layer(2, 0, c)
-        round_and_quantise(2, 1, "f")
+        round_and_quantise(2, 1)
+        picked = gather_words(2, HALF, HALF, "raw01a")
         for c in range(BANKS // 2):
             first_layer(2, 1, c)
-        picked = gather_words(2, HALF, HALF, "f")
-        rounded_down = keep.tile([P, PACK * N], BF16, name="rounded_down", tag="raw2", align_bytes=64)
+        rounded_down = keep.tile([P, PACK * N], BF16, name="rounded_down", align_bytes=64)
         nc.scalar.copy(
             rounded_down[:].rearrange("p (c m u i) -> p m c i u", c=2, u=2, i=PACK),
             raw_down[:].rearrange("p i (m u c) -> p m c i u", u=2, c=2),
@@ -179,27 +177,31 @@ def tile_list_rvq_fff_silu_bias_kernel(tc, tab_words, tab_scales, w0, w1, w2, sm
         down_codes = keep.tile([P, N], U32, name="down_codes", align_bytes=64)
         down_scales = keep.tile([P, N], U8, name="down_scales", align_bytes=64)
         nc.vector.quantize_mx(down_codes[:].bitcast(FP8X4), down_scales[:], rounded_down[:])
-        part_words(2, HALF, picked, "raw2")
+        part_words(2, HALF, picked, "raw00b")
         for c in range(BANKS // 2, BANKS):
             first_layer(2, 0, c)
             first_layer(2, 1, c)
 
 
-        out_rows = out.rearrange("(p c) j -> p c j", p=P)
-        for c0, pair in ((0, 2), (2, 2), (4, 2), (6, 1), (7, 1)):
-            hidden = ring.tile([P, pair, JB, PACK], BF16, name="hidden", align_bytes=64)
-            for c in range(c0, c0 + pair):
-                active = ring.tile([P, JB, PACK], F32, name="active", bufs=BANKS)
-                nc.scalar.activation(active[:], banks[c][:].rearrange("p t j -> p j t"), ACT.Silu)
-                nc.vector.tensor_tensor(hidden[:, c - c0], active[:], smooth_wide[:], ALU.mult)
-            hidden_codes = ring.tile([P, pair * JB], U32, name="hidden_codes", align_bytes=64)
-            hidden_scales = ring.tile([P, pair * JB], U8, name="hidden_scales", align_bytes=64)
-            nc.vector.quantize_mx(hidden_codes[:].bitcast(FP8X4), hidden_scales[:], hidden[:].rearrange("p c j t -> p (c j t)"))
-            y = psum.tile([P, N // P, pair * JB], F32, name=f"y{c0}", tag=f"bank{c0}")
-            result = ring.tile([P, N // P, pair * JB], F32, name="result", bufs=5)
+        active = []
+        for c in range(BANKS):
+            active.append(keep.tile([P, JB, PACK], F32, name=f"active{c}"))
+            nc.scalar.activation(active[c][:], banks[c][:].rearrange("p t j -> p j t"), ACT.Silu)
+
+        hidden = {c0: keep.tile([P, count, JB, PACK], BF16, name=f"hidden{c0}", align_bytes=64) for c0, count in GROUPS}
+        sums = {}
+
+        def smooth_bank(c0, c):
+            nc.vector.tensor_tensor(hidden[c0][:, c - c0], active[c][:], smooth_wide[:], ALU.mult)
+
+        def second_layer(c0, count):
+            hidden_codes = keep.tile([P, count * JB], U32, name=f"hidden_codes{c0}", align_bytes=64)
+            hidden_scales = keep.tile([P, count * JB], U8, name=f"hidden_scales{c0}", align_bytes=64)
+            nc.vector.quantize_mx(hidden_codes[:].bitcast(FP8X4), hidden_scales[:], hidden[c0][:].rearrange("p c j t -> p (c j t)"))
+            sums[c0] = psum.tile([P, N // P, count * JB], F32, name=f"sums{c0}", tag=f"bank{c0}")
             for c in range(N // P):
                 nc.tensor.matmul_mx(
-                    y[:, c, :],
+                    sums[c0][:, c, :],
                     lhsT=down_codes[:, c * P:(c + 1) * P].bitcast(FP8X4),
                     lhsT_scale=down_scales[:, c * P:(c + 1) * P],
                     rhs=hidden_codes[:].bitcast(FP8X4),
@@ -207,6 +209,20 @@ def tile_list_rvq_fff_silu_bias_kernel(tc, tab_words, tab_scales, w0, w1, w2, sm
                     start=True,
                     stop=True,
                 )
+
+        waiting = None
+        for c0, count in GROUPS:
+            smooth_bank(c0, c0)
+            if waiting:
+                second_layer(*waiting)
+            for c in range(c0 + 1, c0 + count):
+                smooth_bank(c0, c)
+            waiting = (c0, count)
+        second_layer(*waiting)
+
+        out_rows = out.rearrange("(p c) j -> p c j", p=P)
+        for c0, count in GROUPS:
+            result = keep.tile([P, N // P, count * JB], F32, name=f"result{c0}")
             for c in range(N // P):
-                nc.scalar.activation(result[:, c, :], y[:, c, :], ACT.Identity, bias=bias[:, c:c + 1])
-            nc.sync.dma_start(out_rows[:, :, c0 * JB:(c0 + pair) * JB], result[:])
+                nc.scalar.activation(result[:, c, :], sums[c0][:, c, :], ACT.Identity, bias=bias[:, c:c + 1])
+            nc.sync.dma_start(out_rows[:, :, c0 * JB:(c0 + count) * JB], result[:])

@@ -19,13 +19,17 @@ ALU = mybir.AluOpType
 P = 128
 PACK = 4
 PASS = P * PACK
-LISTS = 3
 PASSES = K // PASS
+LISTS = 3
+PER_COLUMN = 16
 JB = 128
 BANKS = J // JB
 HALF = J // 2
-GROUPS = ((0, 2), (2, 2), (4, 2), (6, 1), (7, 1))
+PRODUCTS = N // P
+
 RUNS = ((0, 3 * HALF), (3 * HALF, 5 * HALF), (5 * HALF, 6 * HALF))
+
+GROUPS = ((0, 2), (2, 2), (4, 2), (6, 1), (7, 1))
 
 
 def tile_list_rvq_fff_silu_bias_kernel(tc, tab_words, tab_scales, w0, w1, w2, sm, wd, b, offs, out):
@@ -36,152 +40,155 @@ def tile_list_rvq_fff_silu_bias_kernel(tc, tab_words, tab_scales, w0, w1, w2, sm
         keep = ctx.enter_context(tc.tile_pool(name="keep", bufs=1))
         psum = ctx.enter_context(tc.psum_pool(name="psum", bufs=1))
 
-        offsets = keep.tile([P, LISTS * J // 16], U16, name="offsets")
+        offsets = keep.tile([P, LISTS * J // PER_COLUMN], U16, name="offsets")
         table_scales = keep.tile([P, T], U8, name="table_scales", align_bytes=64)
         nc.vector.memset(table_scales[:].bitcast(I32), 0)
-        second_scales = [keep.tile([P, m1 - m0], U8, name=f"second_scales{m0}", align_bytes=64) for m0, m1 in RUNS]
-        for plane in second_scales:
-            nc.gpsimd.memset(plane[:].bitcast(I32), 0)
+        pass1_planes = [keep.tile([P, m1 - m0], U8, name=f"pass1_plane{m0}", align_bytes=64) for m0, m1 in RUNS]
+        for plane in pass1_planes:
+            nc.vector.memset(plane[:].bitcast(I32), 0)
 
         nc.sync.dma_start(offsets[:], offs)
-        smooth = keep.tile([P, 7], F32, name="smooth")
+
+        smooth_run = keep.tile([P, 7], F32, name="smooth_run")
         smooth_rows = sm.rearrange("(c e) -> c e", e=8)
         for u in range(2):
-            nc.sync.dma_start(smooth[u:P:2, :], smooth_rows[:, u:u + 7])
-        smooth_wide = keep.tile([P, JB, PACK], F32, name="smooth_wide")
-        nc.scalar.copy(smooth_wide[:], smooth[:, 0:7:2].unsqueeze(1).to_broadcast([P, JB, PACK]))
-        scale_rows = tab_scales.bitcast(I32).rearrange("a (q r) n -> r q a n", r=4)
+            nc.sync.dma_start(smooth_run[u:P:2, :], smooth_rows[:, u:u + 7])
+        smooth = keep.tile([P, JB, PACK], F32, name="smooth")
+        nc.scalar.copy(smooth[:], smooth_run[:, 0:7:2].unsqueeze(1).to_broadcast([P, JB, PACK]))
+
+        scale_rows = tab_scales.bitcast(I32).rearrange("d (q r) n -> r q d n", r=4)
         for r in range(4):
             nc.sync.dma_start(table_scales[r:P:16, :].bitcast(I32), scale_rows[r])
         table_words = keep.tile([P, T], I32, name="table_words", align_bytes=64)
         nc.sync.dma_start(table_words[:], tab_words[0].rearrange("p t b -> p (t b)").bitcast(I32))
 
-        raw = {}
+        raw, codes, scales, gathered_planes, parted = {}, {}, {}, {}, {}
 
         def load_weight(g, d, tags):
             rows = weights[g][d * PASS:(d + 1) * PASS, :].rearrange("(p i) r -> p i r", i=PACK)
-            parts = len(tags)
-            width = R // parts
+            width = R // len(tags)
             raw[g, d] = []
             for s, tag in enumerate(tags):
                 piece = keep.tile([P, PACK, width], F32, name=f"raw{g}{d}{s}", tag=tag, align_bytes=64)
                 nc.sync.dma_start(piece[:], rows[:, :, s * width:(s + 1) * width])
                 raw[g, d].append(piece)
 
-        load_weight(0, 0, ("raw00a", "raw00b"))
-        load_weight(0, 1, ("raw01a", "raw01b"))
-        load_weight(1, 0, ("raw10",))
-
-        codes, scales = {}, {}
-
         def round_and_quantise(g, d):
             rounded = keep.tile([P, PACK * R], BF16, name=f"rounded{g}{d}", tag=f"rounded{g}{d}", align_bytes=64)
             view = rounded[:].rearrange("p (t c u i) -> p c t i u", t=PACK, u=2, i=PACK)
-            width = P // 2 // len(raw[g, d])
+            pairs = P // 2 // len(raw[g, d])
             for s, piece in enumerate(raw[g, d]):
-                nc.scalar.copy(view[:, s * width:(s + 1) * width], piece[:].rearrange("p i (c t u) -> p c t i u", t=PACK, u=2))
+                nc.scalar.copy(view[:, s * pairs:(s + 1) * pairs], piece[:].rearrange("p i (c t u) -> p c t i u", t=PACK, u=2))
             codes[g, d] = keep.tile([P, R], U32, name=f"codes{g}{d}", align_bytes=64)
             scales[g, d] = keep.tile([P, R], U8, name=f"scales{g}{d}", align_bytes=64)
             nc.vector.quantize_mx(codes[g, d][:].bitcast(FP8X4), scales[g, d][:], rounded[:])
 
-        first_scales = {}
-
-        def gather_scales(s, tag):
-            m0, m1 = RUNS[s]
-            first_scales[s] = keep.tile([P, m1 - m0], U8, name=f"first_scales{s}", tag=tag, align_bytes=64)
-            listed = offsets[:, m0 // 16:m1 // 16]
-            nc.vector.tensor_copy(first_scales[s][:], table_scales[:].indirect(listed))
+        def gather_scales(run, tag):
+            m0, m1 = RUNS[run]
+            gathered_planes[run] = keep.tile([P, m1 - m0], U8, name=f"gathered_plane{run}", tag=tag, align_bytes=64)
+            listed = offsets[:, m0 // PER_COLUMN:m1 // PER_COLUMN]
+            nc.vector.tensor_copy(gathered_planes[run][:], table_scales[:].indirect(listed))
             for r in range(4):
-                nc.sync.dma_start(second_scales[s][r:P:32, :].bitcast(I32), first_scales[s][16 + r:P:32, :].bitcast(I32))
-
-        parted = {}
+                nc.sync.dma_start(pass1_planes[run][r:P:32, :].bitcast(I32), gathered_planes[run][16 + r:P:32, :].bitcast(I32))
 
         def gather_words(g, j0, width, tag):
             picked = keep.tile([P, width], U32, name=f"picked{g}_{j0}", tag=tag, align_bytes=64)
-            listed = offsets[:, (g * J + j0) // 16:(g * J + j0 + width) // 16]
+            listed = offsets[:, (g * J + j0) // PER_COLUMN:(g * J + j0 + width) // PER_COLUMN]
             nc.vector.tensor_copy(picked[:], table_words[:].bitcast(U32).indirect(listed))
             return picked
 
         def part_words(g, j0, picked, tag):
             width = picked.shape[1]
-            halves = keep.tile([P, PASSES, 2 * width], U8, name=f"parted{g}_{j0}", tag=tag, align_bytes=64)
+            by_pass = keep.tile([P, PASSES, 2 * width], U8, name=f"parted{g}_{j0}", tag=tag, align_bytes=64)
             nc.vector.tensor_copy(
-                halves[:].bitcast(U16).rearrange("p d (h j) -> p h d j", h=2),
+                by_pass[:].bitcast(U16).rearrange("p d (h j) -> p h d j", h=2),
                 picked[:].bitcast(U16).rearrange("p (h j d) -> p h d j", h=2, d=PASSES),
             )
             for j in range(j0, j0 + width, JB):
-                parted[g, j // JB] = (halves, j - j0)
+                parted[g, j // JB] = (by_pass, j - j0)
 
         banks = [psum.tile([P, PACK, JB], F32, name=f"bank{c}", tag=f"bank{c}") for c in range(BANKS)]
 
         def first_layer(g, d, c):
-            halves, j0 = parted[g, c]
+            by_pass, j0 = parted[g, c]
             entry = g * J + c * JB
-            s = max(n for n, run in enumerate(RUNS) if run[0] <= entry)
-            m0 = entry - RUNS[s][0]
-            plane = (first_scales, second_scales)[d][s]
+            run = max(n for n, (m0, m1) in enumerate(RUNS) if m0 <= entry)
+            column = entry - RUNS[run][0]
+            plane = (gathered_planes, pass1_planes)[d][run]
             for t in range(PACK):
                 nc.tensor.matmul_mx(
                     banks[c][:, t, :],
                     lhsT=codes[g, d][:, t * P:(t + 1) * P].bitcast(FP8X4),
                     lhsT_scale=scales[g, d][:, t * P:(t + 1) * P],
-                    rhs=halves[:, d, 2 * j0:2 * (j0 + JB)].bitcast(FP4X4),
-                    rhs_scale=plane[:, m0:m0 + JB],
+                    rhs=by_pass[:, d, 2 * j0:2 * (j0 + JB)].bitcast(FP4X4),
+                    rhs_scale=plane[:, column:column + JB],
                     start=(g, d, t) == (0, 0, 0),
                     stop=(g, d, t) == (LISTS - 1, PASSES - 1, PACK - 1),
                 )
 
-        gather_scales(0, "scales0")
+        first_half, second_half = range(BANKS // 2), range(BANKS // 2, BANKS)
+
+        load_weight(0, 0, ("raw00a", "raw00b"))
+        load_weight(0, 1, ("raw01a", "raw01b"))
+        load_weight(1, 0, ("raw10",))
+
+        gather_scales(0, "gathered_plane0")
         part_words(0, 0, gather_words(0, 0, J, "picked0"), "parted0")
         round_and_quantise(0, 0)
         load_weight(1, 1, ("raw00a",))
         load_weight(2, 0, ("rounded00",))
         for c in range(BANKS):
             first_layer(0, 0, c)
+
         picked = gather_words(1, 0, J, "raw00b")
         round_and_quantise(0, 1)
-        load_weight(2, 1, ("raw01a",))
+        load_weight(2, 1, ("raw01a", "rounded01"))
         for c in range(BANKS):
             first_layer(0, 1, c)
+
         part_words(1, 0, picked, "raw01b")
         round_and_quantise(1, 0)
         raw_down = keep.tile([P, PACK, N], F32, name="raw_down", tag="raw00b", align_bytes=64)
         down_rows = wd.rearrange("(c t u) n -> u c t n", t=PACK, u=2)
         for u in range(2):
             nc.sync.dma_start(raw_down[u:P:2], down_rows[u])
-        for c in range(BANKS // 2):
+        for c in first_half:
             first_layer(1, 0, c)
         gather_scales(1, "raw10")
-        for c in range(BANKS // 2, BANKS):
+        for c in second_half:
             first_layer(1, 0, c)
+
         round_and_quantise(1, 1)
-        bias = keep.tile([P, N // P], F32, name="bias", tag="rounded10", align_bytes=64)
+        bias = keep.tile([P, PRODUCTS], F32, name="bias", tag="rounded10", align_bytes=64)
         nc.sync.dma_start(bias[:], b.rearrange("(p c) -> p c", p=P))
         for c in range(BANKS):
             first_layer(1, 1, c)
+
         picked = gather_words(2, 0, HALF, "raw00a")
         round_and_quantise(2, 0)
         part_words(2, 0, picked, "rounded00")
         gather_scales(2, "rounded20")
-        for c in range(BANKS // 2):
+        for c in first_half:
             first_layer(2, 0, c)
+
         round_and_quantise(2, 1)
-        picked = gather_words(2, HALF, HALF, "raw01a")
-        for c in range(BANKS // 2):
+        picked = gather_words(2, HALF, HALF, "rounded01")
+        for c in first_half:
             first_layer(2, 1, c)
+
         rounded_down = keep.tile([P, PACK * N], BF16, name="rounded_down", align_bytes=64)
         nc.scalar.copy(
-            rounded_down[:].rearrange("p (c m u i) -> p m c i u", c=2, u=2, i=PACK),
-            raw_down[:].rearrange("p i (m u c) -> p m c i u", u=2, c=2),
+            rounded_down[:].rearrange("p (c m u t) -> p m c t u", c=PRODUCTS, u=2, t=PACK),
+            raw_down[:].rearrange("p t (m u c) -> p m c t u", u=2, c=PRODUCTS),
         )
         down_codes = keep.tile([P, N], U32, name="down_codes", align_bytes=64)
         down_scales = keep.tile([P, N], U8, name="down_scales", align_bytes=64)
         nc.vector.quantize_mx(down_codes[:].bitcast(FP8X4), down_scales[:], rounded_down[:])
+
         part_words(2, HALF, picked, "raw00b")
-        for c in range(BANKS // 2, BANKS):
+        for c in second_half:
             first_layer(2, 0, c)
             first_layer(2, 1, c)
-
 
         active = []
         for c in range(BANKS):
@@ -192,37 +199,36 @@ def tile_list_rvq_fff_silu_bias_kernel(tc, tab_words, tab_scales, w0, w1, w2, sm
         sums = {}
 
         def smooth_bank(c0, c):
-            nc.vector.tensor_tensor(hidden[c0][:, c - c0], active[c][:], smooth_wide[:], ALU.mult)
+            nc.vector.tensor_tensor(hidden[c0][:, c - c0], active[c][:], smooth[:], ALU.mult)
 
         def second_layer(c0, count):
             hidden_codes = keep.tile([P, count * JB], U32, name=f"hidden_codes{c0}", align_bytes=64)
             hidden_scales = keep.tile([P, count * JB], U8, name=f"hidden_scales{c0}", align_bytes=64)
             nc.vector.quantize_mx(hidden_codes[:].bitcast(FP8X4), hidden_scales[:], hidden[c0][:].rearrange("p c j t -> p (c j t)"))
-            sums[c0] = psum.tile([P, N // P, count * JB], F32, name=f"sums{c0}", tag=f"bank{c0}")
-            for c in range(N // P):
+            sums[c0] = psum.tile([P, PRODUCTS, count * JB], F32, name=f"sums{c0}", tag=f"bank{c0}")
+            for product in range(PRODUCTS):
                 nc.tensor.matmul_mx(
-                    sums[c0][:, c, :],
-                    lhsT=down_codes[:, c * P:(c + 1) * P].bitcast(FP8X4),
-                    lhsT_scale=down_scales[:, c * P:(c + 1) * P],
+                    sums[c0][:, product, :],
+                    lhsT=down_codes[:, product * P:(product + 1) * P].bitcast(FP8X4),
+                    lhsT_scale=down_scales[:, product * P:(product + 1) * P],
                     rhs=hidden_codes[:].bitcast(FP8X4),
                     rhs_scale=hidden_scales[:],
                     start=True,
                     stop=True,
                 )
 
-        waiting = None
-        for c0, count in GROUPS:
+        for n, (c0, count) in enumerate(GROUPS):
             smooth_bank(c0, c0)
-            if waiting:
-                second_layer(*waiting)
+            if n > 0:
+                second_layer(*GROUPS[n - 1])
             for c in range(c0 + 1, c0 + count):
                 smooth_bank(c0, c)
-            waiting = (c0, count)
-        second_layer(*waiting)
+        second_layer(*GROUPS[-1])
 
         out_rows = out.rearrange("(p c) j -> p c j", p=P)
         for c0, count in GROUPS:
-            result = keep.tile([P, N // P, count * JB], F32, name=f"result{c0}")
-            for c in range(N // P):
-                nc.scalar.activation(result[:, c, :], sums[c0][:, c, :], ACT.Identity, bias=bias[:, c:c + 1])
-            nc.sync.dma_start(out_rows[:, :, c0 * JB:(c0 + count) * JB], result[:])
+            result = keep.tile([P, PRODUCTS, count * JB], F32, name=f"result{c0}")
+            for product in range(PRODUCTS):
+                nc.scalar.activation(result[:, product, :], sums[c0][:, product, :], ACT.Identity, bias=bias[:, product:product + 1])
+            queue = nc.scalar if c0 == GROUPS[-1][0] else nc.sync
+            queue.dma_start(out_rows[:, :, c0 * JB:(c0 + count) * JB], result[:])

@@ -28,6 +28,7 @@ HALF = J // 2
 PRODUCTS = N // P
 
 RUNS = ((0, 3 * HALF), (3 * HALF, 5 * HALF), (5 * HALF, 6 * HALF))
+KIB = 1024
 
 GROUPS = ((0, 2), (2, 2), (4, 2), (6, 1), (7, 1))
 
@@ -38,7 +39,11 @@ def tile_list_rvq_fff_silu_bias_kernel(tc, tab_words, tab_scales, w0, w1, w2, sm
 
     with ExitStack() as ctx:
         keep = ctx.enter_context(tc.tile_pool(name="keep", bufs=1))
+        shared = ctx.enter_context(tc.tile_pool(name="shared", bufs=1))
         psum = ctx.enter_context(tc.psum_pool(name="psum", bufs=1))
+
+        def placed(name, shape, dtype, kib):
+            return shared.tile(shape, dtype, name=name, offset=int(kib * KIB), align_bytes=64)
 
         offsets = keep.tile([P, LISTS * J // PER_COLUMN], U16, name="offsets")
         table_scales = keep.tile([P, T], U8, name="table_scales", align_bytes=64)
@@ -59,22 +64,20 @@ def tile_list_rvq_fff_silu_bias_kernel(tc, tab_words, tab_scales, w0, w1, w2, sm
         scale_rows = tab_scales.bitcast(I32).rearrange("d (q r) n -> r q d n", r=4)
         for r in range(4):
             nc.sync.dma_start(table_scales[r:P:16, :].bitcast(I32), scale_rows[r])
-        table_words = keep.tile([P, T], I32, name="table_words", align_bytes=64)
-        nc.sync.dma_start(table_words[:], tab_words[0].rearrange("p t b -> p (t b)").bitcast(I32))
 
         raw, codes, scales, gathered_planes, parted = {}, {}, {}, {}, {}
 
-        def load_weight(g, d, tags):
+        def load_weight(g, d, places):
             rows = weights[g][d * PASS:(d + 1) * PASS, :].rearrange("(p i) r -> p i r", i=PACK)
-            width = R // len(tags)
+            width = R // len(places)
             raw[g, d] = []
-            for s, tag in enumerate(tags):
-                piece = keep.tile([P, PACK, width], F32, name=f"raw{g}{d}{s}", tag=tag, align_bytes=64)
+            for s, kib in enumerate(places):
+                piece = placed(f"raw{g}{d}{s}", [P, PACK, width], F32, kib)
                 nc.sync.dma_start(piece[:], rows[:, :, s * width:(s + 1) * width])
                 raw[g, d].append(piece)
 
-        def round_and_quantise(g, d):
-            rounded = keep.tile([P, PACK * R], BF16, name=f"rounded{g}{d}", tag=f"rounded{g}{d}", align_bytes=64)
+        def round_and_quantise(g, d, kib):
+            rounded = placed(f"rounded{g}{d}", [P, PACK * R], BF16, kib)
             view = rounded[:].rearrange("p (t c u i) -> p c t i u", t=PACK, u=2, i=PACK)
             pairs = P // 2 // len(raw[g, d])
             for s, piece in enumerate(raw[g, d]):
@@ -83,29 +86,37 @@ def tile_list_rvq_fff_silu_bias_kernel(tc, tab_words, tab_scales, w0, w1, w2, sm
             scales[g, d] = keep.tile([P, R], U8, name=f"scales{g}{d}", align_bytes=64)
             nc.vector.quantize_mx(codes[g, d][:].bitcast(FP8X4), scales[g, d][:], rounded[:])
 
-        def gather_scales(run, tag):
+        def gather_scales(run, kib):
             m0, m1 = RUNS[run]
-            gathered_planes[run] = keep.tile([P, m1 - m0], U8, name=f"gathered_plane{run}", tag=tag, align_bytes=64)
+            gathered_planes[run] = placed(f"gathered_plane{run}", [P, m1 - m0], U8, kib)
             listed = offsets[:, m0 // PER_COLUMN:m1 // PER_COLUMN]
             nc.vector.tensor_copy(gathered_planes[run][:], table_scales[:].indirect(listed))
             for r in range(4):
                 nc.sync.dma_start(pass1_planes[run][r:P:32, :].bitcast(I32), gathered_planes[run][16 + r:P:32, :].bitcast(I32))
 
-        def gather_words(g, j0, width, tag):
-            picked = keep.tile([P, width], U32, name=f"picked{g}_{j0}", tag=tag, align_bytes=64)
+        def gather_words(g, j0, width, kib):
+            picked = placed(f"picked{g}_{j0}", [P, width], U32, kib)
             listed = offsets[:, (g * J + j0) // PER_COLUMN:(g * J + j0 + width) // PER_COLUMN]
             nc.vector.tensor_copy(picked[:], table_words[:].bitcast(U32).indirect(listed))
             return picked
 
-        def part_words(g, j0, picked, tag):
+        def part_words(g, j0, picked, kib):
             width = picked.shape[1]
-            by_pass = keep.tile([P, PASSES, 2 * width], U8, name=f"parted{g}_{j0}", tag=tag, align_bytes=64)
+            by_pass = placed(f"parted{g}_{j0}", [P, PASSES, 2 * width], U8, kib)
             nc.vector.tensor_copy(
                 by_pass[:].bitcast(U16).rearrange("p d (h j) -> p h d j", h=2),
                 picked[:].bitcast(U16).rearrange("p (h j d) -> p h d j", h=2, d=PASSES),
             )
             for j in range(j0, j0 + width, JB):
                 parted[g, j // JB] = (by_pass, j - j0)
+
+        def gather_pieces(g, j0, widths, kib):
+            starts = [j0 + sum(widths[:n]) for n in range(len(widths))]
+            return [(j, gather_words(g, j, width, kib + (j - j0) * 4 / KIB)) for j, width in zip(starts, widths)]
+
+        def part_pieces(g, pieces, kib):
+            for j, picked in pieces:
+                part_words(g, j, picked, kib + (j - pieces[0][0]) * 4 / KIB)
 
         banks = [psum.tile([P, PACK, JB], F32, name=f"bank{c}", tag=f"bank{c}") for c in range(BANKS)]
 
@@ -128,51 +139,58 @@ def tile_list_rvq_fff_silu_bias_kernel(tc, tab_words, tab_scales, w0, w1, w2, sm
 
         first_half, second_half = range(BANKS // 2), range(BANKS // 2, BANKS)
 
-        load_weight(0, 0, ("raw00a", "raw00b"))
-        load_weight(0, 1, ("raw01a", "raw01b"))
-        load_weight(1, 0, ("raw10",))
+        RAW00A, RAW00B, RAW01A, RAW01B, RAW10, ROUNDED00, ROUNDED01 = 0, 8, 12, 16, 20, 28, 36
+        ROUNDED10, ROUNDED11, ROUNDED20, ROUNDED21, PLANE0, PICKED0, PARTED0 = 40, 44, 48, 52, 56, 58, 62
+        RAW11, RAW20, RAW21A, RAW21B, RAW_DOWN = RAW00A, ROUNDED00, RAW01A, ROUNDED01, RAW00B
+        quarter = 2 * JB
 
-        gather_scales(0, "gathered_plane0")
-        part_words(0, 0, gather_words(0, 0, J, "picked0"), "parted0")
-        round_and_quantise(0, 0)
-        load_weight(1, 1, ("raw00a",))
-        load_weight(2, 0, ("rounded00",))
+        table_words = keep.tile([P, T], I32, name="table_words", align_bytes=64)
+        nc.sync.dma_start(table_words[:], tab_words[0].rearrange("p t b -> p (t b)").bitcast(I32))
+        load_weight(0, 0, (RAW00A, RAW00B))
+        load_weight(0, 1, (RAW01A, RAW01B))
+        load_weight(1, 0, (RAW10,))
+
+        gather_scales(0, PLANE0)
+        part_pieces(0, gather_pieces(0, 0, [quarter] * 4, PICKED0), PARTED0)
+        round_and_quantise(0, 0, ROUNDED00)
+        load_weight(1, 1, (RAW11,))
+        load_weight(2, 0, (RAW20,))
         for c in range(BANKS):
             first_layer(0, 0, c)
 
-        picked = gather_words(1, 0, J, "raw00b")
-        round_and_quantise(0, 1)
-        load_weight(2, 1, ("raw01a", "rounded01"))
+        pieces = gather_pieces(1, 0, [HALF] * 2, RAW00B)
+        round_and_quantise(0, 1, ROUNDED01)
+        load_weight(2, 1, (RAW21A, RAW21B))
         for c in range(BANKS):
             first_layer(0, 1, c)
 
-        part_words(1, 0, picked, "raw01b")
-        round_and_quantise(1, 0)
-        raw_down = keep.tile([P, PACK, N], F32, name="raw_down", tag="raw00b", align_bytes=64)
+        part_pieces(1, pieces, RAW01B)
+        round_and_quantise(1, 0, ROUNDED10)
+        raw_down = placed("raw_down", [P, PACK, N], F32, RAW_DOWN)
         down_rows = wd.rearrange("(c t u) n -> u c t n", t=PACK, u=2)
         for u in range(2):
             nc.sync.dma_start(raw_down[u:P:2], down_rows[u])
         for c in first_half:
             first_layer(1, 0, c)
-        gather_scales(1, "raw10")
+        gather_scales(1, RAW10)
         for c in second_half:
             first_layer(1, 0, c)
 
-        round_and_quantise(1, 1)
-        bias = keep.tile([P, PRODUCTS], F32, name="bias", tag="rounded10", align_bytes=64)
+        round_and_quantise(1, 1, ROUNDED11)
+        bias = placed("bias", [P, PRODUCTS], F32, ROUNDED10)
         nc.sync.dma_start(bias[:], b.rearrange("(p c) -> p c", p=P))
         for c in range(BANKS):
             first_layer(1, 1, c)
 
-        picked = gather_words(2, 0, HALF, "raw00a")
-        round_and_quantise(2, 0)
-        part_words(2, 0, picked, "rounded00")
-        gather_scales(2, "rounded20")
+        pieces = gather_pieces(2, 0, [quarter] * 2, RAW11)
+        round_and_quantise(2, 0, ROUNDED20)
+        part_pieces(2, pieces, RAW20)
+        gather_scales(2, RAW20 + 2)
         for c in first_half:
             first_layer(2, 0, c)
 
-        round_and_quantise(2, 1)
-        picked = gather_words(2, HALF, HALF, "rounded01")
+        round_and_quantise(2, 1, ROUNDED21)
+        pieces = gather_pieces(2, HALF, [quarter, JB, JB], RAW21B)
         for c in first_half:
             first_layer(2, 1, c)
 
@@ -185,7 +203,7 @@ def tile_list_rvq_fff_silu_bias_kernel(tc, tab_words, tab_scales, w0, w1, w2, sm
         down_scales = keep.tile([P, N], U8, name="down_scales", align_bytes=64)
         nc.vector.quantize_mx(down_codes[:].bitcast(FP8X4), down_scales[:], rounded_down[:])
 
-        part_words(2, HALF, picked, "raw00b")
+        part_pieces(2, pieces, RAW_DOWN)
         for c in second_half:
             first_layer(2, 0, c)
             first_layer(2, 1, c)

@@ -46,19 +46,19 @@ def tile_list_rvq_fff_silu_bias_kernel(tc, tab_words, tab_scales, w0, w1, w2, sm
             return shared.tile(shape, dtype, name=name, offset=int(kib * KIB), align_bytes=64)
 
         offsets = keep.tile([P, LISTS * J // PER_COLUMN], U16, name="offsets")
-        table_scales = keep.tile([P, T], U8, name="table_scales", align_bytes=64)
+        table_scales = placed("table_scales", [P, T], U8, 0)
         nc.vector.memset(table_scales[:].bitcast(I32), 0)
-        pass1_planes = [keep.tile([P, m1 - m0], U8, name=f"pass1_plane{m0}", align_bytes=64) for m0, m1 in RUNS]
+        pass1_planes = [placed(f"pass1_plane{m0}", [P, m1 - m0], U8, 224 + m0 / KIB) for m0, m1 in RUNS]
         for plane in pass1_planes:
             nc.vector.memset(plane[:].bitcast(I32), 0)
 
         nc.sync.dma_start(offsets[:], offs)
 
-        smooth_run = keep.tile([P, 7], F32, name="smooth_run")
+        smooth_run = placed("smooth_run", [P, 7], F32, 10)
         smooth_rows = sm.rearrange("(c e) -> c e", e=8)
         for u in range(2):
             nc.sync.dma_start(smooth_run[u:P:2, :], smooth_rows[:, u:u + 7])
-        smooth = keep.tile([P, JB, PACK], F32, name="smooth")
+        smooth = placed("smooth", [P, JB, PACK], F32, 11)
         nc.scalar.copy(smooth[:], smooth_run[:, 0:7:2].unsqueeze(1).to_broadcast([P, JB, PACK]))
 
         scale_rows = tab_scales.bitcast(I32).rearrange("d (q r) n -> r q d n", r=4)
@@ -82,8 +82,8 @@ def tile_list_rvq_fff_silu_bias_kernel(tc, tab_words, tab_scales, w0, w1, w2, sm
             pairs = P // 2 // len(raw[g, d])
             for s, piece in enumerate(raw[g, d]):
                 nc.scalar.copy(view[:, s * pairs:(s + 1) * pairs], piece[:].rearrange("p i (c t u) -> p c t i u", t=PACK, u=2))
-            codes[g, d] = keep.tile([P, R], U32, name=f"codes{g}{d}", align_bytes=64)
-            scales[g, d] = keep.tile([P, R], U8, name=f"scales{g}{d}", align_bytes=64)
+            codes[g, d] = placed(f"codes{g}{d}", [P, R], U32, 128 + 2.5 * (2 * g + d))
+            scales[g, d] = placed(f"scales{g}{d}", [P, R], U8, 130 + 2.5 * (2 * g + d))
             nc.vector.quantize_mx(codes[g, d][:].bitcast(FP8X4), scales[g, d][:], rounded[:])
 
         def gather_scales(run, kib):
@@ -139,12 +139,12 @@ def tile_list_rvq_fff_silu_bias_kernel(tc, tab_words, tab_scales, w0, w1, w2, sm
 
         first_half, second_half = range(BANKS // 2), range(BANKS // 2, BANKS)
 
-        RAW00A, RAW00B, RAW01A, RAW01B, RAW10, ROUNDED00, ROUNDED01 = 0, 8, 12, 16, 20, 28, 36
-        ROUNDED10, ROUNDED11, ROUNDED20, ROUNDED21, PLANE0, PICKED0, PARTED0 = 40, 44, 48, 52, 56, 58, 62
+        RAW00A, RAW00B, RAW01A, RAW01B, RAW10, ROUNDED00, ROUNDED01 = 64, 72, 76, 80, 84, 92, 100
+        ROUNDED10, ROUNDED11, ROUNDED20, ROUNDED21, PLANE0, PICKED0, PARTED0 = 192, 196, 200, 204, 208, 210, 214
         RAW11, RAW20, RAW21A, RAW21B, RAW_DOWN = RAW00A, ROUNDED00, RAW01A, ROUNDED01, RAW00B
         quarter = 2 * JB
 
-        table_words = keep.tile([P, T], I32, name="table_words", align_bytes=64)
+        table_words = placed("table_words", [P, T], I32, 2)
         nc.sync.dma_start(table_words[:], tab_words[0].rearrange("p t b -> p (t b)").bitcast(I32))
         load_weight(0, 0, (RAW00A, RAW00B))
         load_weight(0, 1, (RAW01A, RAW01B))
@@ -194,13 +194,13 @@ def tile_list_rvq_fff_silu_bias_kernel(tc, tab_words, tab_scales, w0, w1, w2, sm
         for c in first_half:
             first_layer(2, 1, c)
 
-        rounded_down = keep.tile([P, PACK * N], BF16, name="rounded_down", align_bytes=64)
+        rounded_down = placed("rounded_down", [P, PACK * N], BF16, 218)
         nc.scalar.copy(
             rounded_down[:].rearrange("p (c m u t) -> p m c t u", c=PRODUCTS, u=2, t=PACK),
             raw_down[:].rearrange("p t (m u c) -> p m c t u", u=2, c=PRODUCTS),
         )
-        down_codes = keep.tile([P, N], U32, name="down_codes", align_bytes=64)
-        down_scales = keep.tile([P, N], U8, name="down_scales", align_bytes=64)
+        down_codes = placed("down_codes", [P, N], U32, 143)
+        down_scales = placed("down_scales", [P, N], U8, 144)
         nc.vector.quantize_mx(down_codes[:].bitcast(FP8X4), down_scales[:], rounded_down[:])
 
         part_pieces(2, pieces, RAW_DOWN)
@@ -210,18 +210,18 @@ def tile_list_rvq_fff_silu_bias_kernel(tc, tab_words, tab_scales, w0, w1, w2, sm
 
         active = []
         for c in range(BANKS):
-            active.append(keep.tile([P, JB, PACK], F32, name=f"active{c}"))
+            active.append(placed(f"active{c}", [P, JB, PACK], F32, 13 + 2 * c))
             nc.scalar.activation(active[c][:], banks[c][:].rearrange("p t j -> p j t"), ACT.Silu)
 
-        hidden = {c0: keep.tile([P, count, JB, PACK], BF16, name=f"hidden{c0}", align_bytes=64) for c0, count in GROUPS}
+        hidden = {c0: placed(f"hidden{c0}", [P, count, JB, PACK], BF16, 150 + c0) for c0, count in GROUPS}
         sums = {}
 
         def smooth_bank(c0, c):
             nc.vector.tensor_tensor(hidden[c0][:, c - c0], active[c][:], smooth[:], ALU.mult)
 
         def second_layer(c0, count):
-            hidden_codes = keep.tile([P, count * JB], U32, name=f"hidden_codes{c0}", align_bytes=64)
-            hidden_scales = keep.tile([P, count * JB], U8, name=f"hidden_scales{c0}", align_bytes=64)
+            hidden_codes = placed(f"hidden_codes{c0}", [P, count * JB], U32, 29 + c0 / 2)
+            hidden_scales = placed(f"hidden_scales{c0}", [P, count * JB], U8, 33 + c0 / 8)
             nc.vector.quantize_mx(hidden_codes[:].bitcast(FP8X4), hidden_scales[:], hidden[c0][:].rearrange("p c j t -> p (c j t)"))
             sums[c0] = psum.tile([P, PRODUCTS, count * JB], F32, name=f"sums{c0}", tag=f"bank{c0}")
             for product in range(PRODUCTS):
@@ -245,7 +245,7 @@ def tile_list_rvq_fff_silu_bias_kernel(tc, tab_words, tab_scales, w0, w1, w2, sm
 
         out_rows = out.rearrange("(p c) j -> p c j", p=P)
         for c0, count in GROUPS:
-            result = keep.tile([P, PRODUCTS, count * JB], F32, name=f"result{c0}")
+            result = placed(f"result{c0}", [P, PRODUCTS, count * JB], F32, 160 + c0)
             for product in range(PRODUCTS):
                 nc.scalar.activation(result[:, product, :], sums[c0][:, product, :], ACT.Identity, bias=bias[:, product:product + 1])
             queue = nc.scalar if c0 == GROUPS[-1][0] else nc.sync

@@ -54,6 +54,11 @@ def tile_list_rvq_fff_silu_bias_kernel(tc, tab_words, tab_scales, w0, w1, w2, sm
 
         nc.sync.dma_start(offsets[:], offs)
 
+        warm_in = placed("warm_in", [P, 1], F32, 230)
+        warm_out = placed("warm_out", [P, 1], F32, 231)
+        nc.vector.memset(warm_in[:], 0.0)
+        nc.scalar.activation(warm_out[:], warm_in[:], ACT.Silu)
+
         smooth_run = placed("smooth_run", [P, 7], F32, 10)
         smooth_rows = sm.rearrange("(c e) -> c e", e=8)
         for u in range(2):
@@ -134,7 +139,7 @@ def tile_list_rvq_fff_silu_bias_kernel(tc, tab_words, tab_scales, w0, w1, w2, sm
                     rhs=by_pass[:, d, 2 * j0:2 * (j0 + JB)].bitcast(FP4X4),
                     rhs_scale=plane[:, column:column + JB],
                     start=(g, d, t) == (0, 0, 0),
-                    stop=(g, d, t) == (LISTS - 1, PASSES - 1, PACK - 1),
+                    stop=(g, d, t) == (LISTS - 1, 0, PACK - 1),
                 )
 
         first_half, second_half = range(BANKS // 2), range(BANKS // 2, BANKS)
@@ -186,13 +191,12 @@ def tile_list_rvq_fff_silu_bias_kernel(tc, tab_words, tab_scales, w0, w1, w2, sm
         round_and_quantise(2, 0, ROUNDED20)
         part_pieces(2, pieces, RAW20)
         gather_scales(2, RAW20 + 2)
-        for c in first_half:
-            first_layer(2, 0, c)
 
         round_and_quantise(2, 1, ROUNDED21)
         pieces = gather_pieces(2, HALF, [quarter, JB, JB], RAW21B)
         for c in first_half:
             first_layer(2, 1, c)
+            first_layer(2, 0, c)
 
         rounded_down = placed("rounded_down", [P, PACK * N], BF16, 218)
         nc.scalar.copy(
@@ -205,8 +209,8 @@ def tile_list_rvq_fff_silu_bias_kernel(tc, tab_words, tab_scales, w0, w1, w2, sm
 
         part_pieces(2, pieces, RAW_DOWN)
         for c in second_half:
-            first_layer(2, 0, c)
             first_layer(2, 1, c)
+            first_layer(2, 0, c)
 
         active = []
         for c in range(BANKS):

@@ -27,7 +27,7 @@ BANKS = J // JB
 HALF = J // 2
 PRODUCTS = N // P
 
-RUNS = ((0, 3 * HALF), (3 * HALF, 5 * HALF), (5 * HALF, 6 * HALF))
+RUNS = ((0, 14 * JB), (14 * JB, 20 * JB), (20 * JB, 24 * JB))
 KIB = 1024
 
 GROUPS = ((0, 2), (2, 2), (4, 2), (6, 1), (7, 1))
@@ -77,8 +77,9 @@ def tile_list_rvq_fff_silu_bias_kernel(tc, tab_words, tab_scales, w0, w1, w2, sm
             width = R // len(places)
             raw[g, d] = []
             for s, kib in enumerate(places):
-                piece = placed(f"raw{g}{d}{s}", [P, PACK, width], F32, kib)
-                nc.sync.dma_start(piece[:], rows[:, :, s * width:(s + 1) * width])
+                room = PACK + 2 if (g, d, s) == (0, 0, 1) else PACK
+                piece = placed(f"raw{g}{d}{s}", [P, room, width], F32, kib)[:, :PACK, :]
+                nc.sync.dma_start(piece, rows[:, :, s * width:(s + 1) * width])
                 raw[g, d].append(piece)
 
         def round_and_quantise(g, d, kib):
@@ -86,7 +87,7 @@ def tile_list_rvq_fff_silu_bias_kernel(tc, tab_words, tab_scales, w0, w1, w2, sm
             view = rounded[:].rearrange("p (t c u i) -> p c t i u", t=PACK, u=2, i=PACK)
             pairs = P // 2 // len(raw[g, d])
             for s, piece in enumerate(raw[g, d]):
-                nc.scalar.copy(view[:, s * pairs:(s + 1) * pairs], piece[:].rearrange("p i (c t u) -> p c t i u", t=PACK, u=2))
+                nc.scalar.copy(view[:, s * pairs:(s + 1) * pairs], piece.rearrange("p i (c t u) -> p c t i u", t=PACK, u=2))
             codes[g, d] = placed(f"codes{g}{d}", [P, R], U32, 128 + 2.5 * (2 * g + d))
             scales[g, d] = placed(f"scales{g}{d}", [P, R], U8, 130 + 2.5 * (2 * g + d))
             nc.vector.quantize_mx(codes[g, d][:].bitcast(FP8X4), scales[g, d][:], rounded[:])
@@ -94,8 +95,10 @@ def tile_list_rvq_fff_silu_bias_kernel(tc, tab_words, tab_scales, w0, w1, w2, sm
         def gather_scales(run, kib):
             m0, m1 = RUNS[run]
             gathered_planes[run] = placed(f"gathered_plane{run}", [P, m1 - m0], U8, kib)
-            listed = offsets[:, m0 // PER_COLUMN:m1 // PER_COLUMN]
-            nc.vector.tensor_copy(gathered_planes[run][:], table_scales[:].indirect(listed))
+            for start in range(m0, m1, J):
+                stop = min(start + J, m1)
+                listed = offsets[:, start // PER_COLUMN:stop // PER_COLUMN]
+                nc.vector.tensor_copy(gathered_planes[run][:, start - m0:stop - m0], table_scales[:].indirect(listed))
             for r in range(4):
                 nc.sync.dma_start(pass1_planes[run][r:P:32, :].bitcast(I32), gathered_planes[run][16 + r:P:32, :].bitcast(I32))
 
@@ -144,7 +147,7 @@ def tile_list_rvq_fff_silu_bias_kernel(tc, tab_words, tab_scales, w0, w1, w2, sm
 
         first_half, second_half = range(BANKS // 2), range(BANKS // 2, BANKS)
 
-        RAW00A, RAW00B, RAW01A, RAW01B, RAW10, ROUNDED00, ROUNDED01 = 64, 72, 76, 80, 84, 92, 100
+        RAW00A, RAW00B, RAW01A, RAW01B, RAW10, ROUNDED00, ROUNDED01 = 64, 72, 78, 82, 86, 94, 102
         ROUNDED10, ROUNDED11, ROUNDED20, ROUNDED21, PLANE0, PICKED0, PARTED0 = 192, 196, 200, 204, 208, 210, 214
         RAW11, RAW20, RAW21A, RAW21B, RAW_DOWN = RAW00A, ROUNDED00, RAW01A, ROUNDED01, RAW00B
         quarter = 2 * JB
@@ -156,8 +159,10 @@ def tile_list_rvq_fff_silu_bias_kernel(tc, tab_words, tab_scales, w0, w1, w2, sm
         load_weight(1, 0, (RAW10,))
 
         gather_scales(0, PLANE0)
-        part_pieces(0, gather_pieces(0, 0, [quarter] * 4, PICKED0), PARTED0)
+        pieces = gather_pieces(0, 0, [quarter] * 4, PICKED0)
+        part_pieces(0, pieces[:2], PARTED0)
         round_and_quantise(0, 0, ROUNDED00)
+        part_pieces(0, pieces[2:], RAW00B + 4)
         load_weight(1, 1, (RAW11,))
         load_weight(2, 0, (RAW20,))
         for c in range(BANKS):
@@ -175,22 +180,23 @@ def tile_list_rvq_fff_silu_bias_kernel(tc, tab_words, tab_scales, w0, w1, w2, sm
         down_rows = wd.rearrange("(c t u) n -> u c t n", t=PACK, u=2)
         for u in range(2):
             nc.sync.dma_start(raw_down[u:P:2], down_rows[u])
-        for c in first_half:
+        for c in range(6):
             first_layer(1, 0, c)
         gather_scales(1, RAW10)
-        for c in second_half:
+        for c in range(6, BANKS):
             first_layer(1, 0, c)
 
+        pieces = gather_pieces(2, 0, [quarter], RAW10 + 1)
         round_and_quantise(1, 1, ROUNDED11)
         bias = placed("bias", [P, PRODUCTS], F32, ROUNDED10)
         nc.sync.dma_start(bias[:], b.rearrange("(p c) -> p c", p=P))
         for c in range(BANKS):
             first_layer(1, 1, c)
 
-        pieces = gather_pieces(2, 0, [quarter] * 2, RAW11)
+        pieces.extend(gather_pieces(2, quarter, [quarter], RAW11))
+        gather_scales(2, RAW11 + 2)
         round_and_quantise(2, 0, ROUNDED20)
         part_pieces(2, pieces, RAW20)
-        gather_scales(2, RAW20 + 2)
 
         round_and_quantise(2, 1, ROUNDED21)
         pieces = gather_pieces(2, HALF, [quarter, JB, JB], RAW21B)

@@ -54,11 +54,6 @@ def tile_list_rvq_fff_silu_bias_kernel(tc, tab_words, tab_scales, w0, w1, w2, sm
 
         nc.sync.dma_start(offsets[:], offs)
 
-        warm_in = placed("warm_in", [P, 1], F32, 230)
-        warm_out = placed("warm_out", [P, 1], F32, 231)
-        nc.vector.memset(warm_in[:], 0.0)
-        nc.scalar.activation(warm_out[:], warm_in[:], ACT.Silu)
-
         smooth_run = placed("smooth_run", [P, 7], F32, 10)
         smooth_rows = sm.rearrange("(c e) -> c e", e=8)
         for u in range(2):

@@ -154,10 +154,10 @@ def tile_list_rvq_fff_silu_bias_kernel(tc, tab_words, tab_scales, w0, w1, w2, sm
         load_weight(1, 0, (RAW10,))
 
         gather_scales(0, PLANE0)
-        pieces = gather_pieces(0, 0, [quarter] * 4, PICKED0)
-        part_pieces(0, pieces[:2], PARTED0)
+        pieces = gather_pieces(0, 0, [HALF] * 2, PICKED0)
+        part_pieces(0, pieces[:1], PARTED0)
         round_and_quantise(0, 0, ROUNDED00)
-        part_pieces(0, pieces[2:], RAW00B + 4)
+        part_pieces(0, pieces[1:], RAW00B + 4)
         load_weight(1, 1, (RAW11,))
         load_weight(2, 0, (RAW20,))
         for c in range(BANKS):
@@ -181,14 +181,13 @@ def tile_list_rvq_fff_silu_bias_kernel(tc, tab_words, tab_scales, w0, w1, w2, sm
         for c in range(6, BANKS):
             first_layer(1, 0, c)
 
-        pieces = gather_pieces(2, 0, [quarter], RAW10 + 1)
         round_and_quantise(1, 1, ROUNDED11)
         bias = placed("bias", [P, PRODUCTS], F32, ROUNDED10)
         nc.sync.dma_start(bias[:], b.rearrange("(p c) -> p c", p=P))
         for c in range(BANKS):
             first_layer(1, 1, c)
 
-        pieces.extend(gather_pieces(2, quarter, [quarter], RAW11))
+        pieces = gather_pieces(2, 0, [HALF], RAW11)
         gather_scales(2, RAW11 + 2)
         round_and_quantise(2, 0, ROUNDED20)
         part_pieces(2, pieces, RAW20)
@@ -228,10 +227,14 @@ def tile_list_rvq_fff_silu_bias_kernel(tc, tab_words, tab_scales, w0, w1, w2, sm
             hidden_codes = placed(f"hidden_codes{c0}", [P, count * JB], U32, 29 + c0 / 2)
             hidden_scales = placed(f"hidden_scales{c0}", [P, count * JB], U8, 33 + c0 / 8)
             nc.vector.quantize_mx(hidden_codes[:].bitcast(FP8X4), hidden_scales[:], hidden[c0][:].rearrange("p c j t -> p (c j t)"))
-            sums[c0] = psum.tile([P, PRODUCTS, count * JB], F32, name=f"sums{c0}", tag=f"bank{c0}")
+            if c0 == BANKS - 1:
+                sums[c0] = [psum.tile([P, JB], F32, name=f"last_sums{n}", tag=f"bank{bank}")[:] for n, bank in enumerate((c0, 1))]
+            else:
+                both = psum.tile([P, PRODUCTS, count * JB], F32, name=f"sums{c0}", tag=f"bank{c0}")
+                sums[c0] = [both[:, product, :] for product in range(PRODUCTS)]
             for product in range(PRODUCTS):
                 nc.tensor.matmul_mx(
-                    sums[c0][:, product, :],
+                    sums[c0][product],
                     lhsT=down_codes[:, product * P:(product + 1) * P].bitcast(FP8X4),
                     lhsT_scale=down_scales[:, product * P:(product + 1) * P],
                     rhs=hidden_codes[:].bitcast(FP8X4),
@@ -252,6 +255,9 @@ def tile_list_rvq_fff_silu_bias_kernel(tc, tab_words, tab_scales, w0, w1, w2, sm
         for c0, count in GROUPS:
             result = placed(f"result{c0}", [P, PRODUCTS, count * JB], F32, 160 + c0)
             for product in range(PRODUCTS):
-                nc.scalar.activation(result[:, product, :], sums[c0][:, product, :], ACT.Identity, bias=bias[:, product:product + 1])
+                if (c0, product) == (BANKS - 1, 0):
+                    nc.vector.tensor_scalar_add(result[:, product, :], sums[c0][product], bias[:, product:product + 1])
+                else:
+                    nc.scalar.activation(result[:, product, :], sums[c0][product], ACT.Identity, bias=bias[:, product:product + 1])
             queue = nc.scalar if c0 == GROUPS[-1][0] else nc.sync
             queue.dma_start(out_rows[:, :, c0 * JB:(c0 + count) * JB], result[:])

from contextlib import ExitStack

import concourse.mybir as mybir

K, R, N, T, J = 1024, 512, 256, 2048, 1024
FLOPS = 2 * (3 * K * R * J + R * N * J)

F32 = mybir.dt.float32
BF16 = mybir.dt.bfloat16
I32 = mybir.dt.int32
U32 = mybir.dt.uint32
U16 = mybir.dt.uint16
U8 = mybir.dt.uint8
FP8X4 = mybir.dt.float8_e4m3fn_x4
FP4X4 = mybir.dt.float4_e2m1fn_x4
ACT = mybir.ActivationFunctionType
ALU = mybir.AluOpType

P = 128
PACK = 4
PASS = P * PACK
PASSES = K // PASS
LISTS = 3
PER_COLUMN = 16
JB = 128
BANKS = J // JB
HALF = J // 2
PRODUCTS = N // P

RUNS = ((0, 14 * JB), (14 * JB, 20 * JB), (20 * JB, 24 * JB))
KIB = 1024

GROUPS = ((0, 2), (2, 2), (4, 2), (6, 1), (7, 1))


def tile_list_rvq_fff_silu_bias_kernel(tc, tab_words, tab_scales, w0, w1, w2, sm, wd, b, offs, out):
    nc = tc.nc
    weights = (w0, w1, w2)

    with ExitStack() as ctx:
        keep = ctx.enter_context(tc.tile_pool(name="keep", bufs=1))
        shared = ctx.enter_context(tc.tile_pool(name="shared", bufs=1))
        psum = ctx.enter_context(tc.psum_pool(name="psum", bufs=1))

        def placed(name, shape, dtype, kib):
            return shared.tile(shape, dtype, name=name, offset=int(kib * KIB), align_bytes=64)

        offsets = keep.tile([P, LISTS * J // PER_COLUMN], U16, name="offsets")
        table_scales = placed("table_scales", [P, T], U8, 0)
        nc.vector.memset(table_scales[:].bitcast(I32), 0)
        pass1_planes = [placed(f"pass1_plane{m0}", [P, m1 - m0], U8, 224 + m0 / KIB) for m0, m1 in RUNS]
        for plane in pass1_planes:
            nc.vector.memset(plane[:].bitcast(I32), 0)

        nc.sync.dma_start(offsets[:], offs)

        smooth_run = placed("smooth_run", [P, 7], F32, 10)
        smooth_rows = sm.rearrange("(c e) -> c e", e=8)
        for u in range(2):
            nc.sync.dma_start(smooth_run[u:P:2, :], smooth_rows[:, u:u + 7])
        smooth = placed("smooth", [P, JB, PACK], F32, 11)
        nc.scalar.copy(smooth[:], smooth_run[:, 0:7:2].unsqueeze(1).to_broadcast([P, JB, PACK]))

        scale_rows = tab_scales.bitcast(I32).rearrange("d (q r) n -> r q d n", r=4)
        for r in range(4):
            nc.sync.dma_start(table_scales[r:P:16, :].bitcast(I32), scale_rows[r])

        raw, codes, scales, gathered_planes, parted = {}, {}, {}, {}, {}

        def load_weight(g, d, places):
            rows = weights[g][d * PASS:(d + 1) * PASS, :].rearrange("(p i) r -> p i r", i=PACK)
            width = R // len(places)
            raw[g, d] = []
            for s, kib in enumerate(places):
                room = PACK + 2 if (g, d, s) == (0, 0, 1) else PACK
                piece = placed(f"raw{g}{d}{s}", [P, room, width], F32, kib)[:, :PACK, :]
                nc.sync.dma_start(piece, rows[:, :, s * width:(s + 1) * width])
                raw[g, d].append(piece)

        def round_and_quantise(g, d, kib):
            rounded = placed(f"rounded{g}{d}", [P, PACK * R], BF16, kib)
            view = rounded[:].rearrange("p (t c u i) -> p c t i u", t=PACK, u=2, i=PACK)
            pairs = P // 2 // len(raw[g, d])
            for s, piece in enumerate(raw[g, d]):
                nc.scalar.copy(view[:, s * pairs:(s + 1) * pairs], piece.rearrange("p i (c t u) -> p c t i u", t=PACK, u=2))
            codes[g, d] = placed(f"codes{g}{d}", [P, R], U32, 128 + 2.5 * (2 * g + d))
            scales[g, d] = placed(f"scales{g}{d}", [P, R], U8, 130 + 2.5 * (2 * g + d))
            nc.vector.quantize_mx(codes[g, d][:].bitcast(FP8X4), scales[g, d][:], rounded[:])

        def gather_scales(run, kib):
            m0, m1 = RUNS[run]
            gathered_planes[run] = placed(f"gathered_plane{run}", [P, m1 - m0], U8, kib)
            for start in range(m0, m1, J):
                stop = min(start + J, m1)
                listed = offsets[:, start // PER_COLUMN:stop // PER_COLUMN]
                nc.vector.tensor_copy(gathered_planes[run][:, start - m0:stop - m0], table_scales[:].indirect(listed))
            for r in range(4):
                nc.sync.dma_start(pass1_planes[run][r:P:32, :].bitcast(I32), gathered_planes[run][16 + r:P:32, :].bitcast(I32))

        def gather_words(g, j0, width, kib):
            picked = placed(f"picked{g}_{j0}", [P, width], U32, kib)
            listed = offsets[:, (g * J + j0) // PER_COLUMN:(g * J + j0 + width) // PER_COLUMN]
            nc.vector.tensor_copy(picked[:], table_words[:].bitcast(U32).indirect(listed))
            return picked

        def part_words(g, j0, picked, kib):
            width = picked.shape[1]
            by_pass = placed(f"parted{g}_{j0}", [P, PASSES, 2 * width], U8, kib)
            nc.vector.tensor_copy(
                by_pass[:].bitcast(U16).rearrange("p d (h j) -> p h d j", h=2),
                picked[:].bitcast(U16).rearrange("p (h j d) -> p h d j", h=2, d=PASSES),
            )
            for j in range(j0, j0 + width, JB):
                parted[g, j // JB] = (by_pass, j - j0)

        def gather_pieces(g, j0, widths, kib):
            starts = [j0 + sum(widths[:n]) for n in range(len(widths))]
            return [(j, gather_words(g, j, width, kib + (j - j0) * 4 / KIB)) for j, width in zip(starts, widths)]

        def part_pieces(g, pieces, kib):
            for j, picked in pieces:
                part_words(g, j, picked, kib + (j - pieces[0][0]) * 4 / KIB)

        banks = [psum.tile([P, PACK, JB], F32, name=f"bank{c}", tag=f"bank{c}") for c in range(BANKS)]

        def first_layer(g, d, c):
            by_pass, j0 = parted[g, c]
            entry = g * J + c * JB
            run = max(n for n, (m0, m1) in enumerate(RUNS) if m0 <= entry)
            column = entry - RUNS[run][0]
            plane = (gathered_planes, pass1_planes)[d][run]
            for t in range(PACK):
                nc.tensor.matmul_mx(
                    banks[c][:, t, :],
                    lhsT=codes[g, d][:, t * P:(t + 1) * P].bitcast(FP8X4),
                    lhsT_scale=scales[g, d][:, t * P:(t + 1) * P],
                    rhs=by_pass[:, d, 2 * j0:2 * (j0 + JB)].bitcast(FP4X4),
                    rhs_scale=plane[:, column:column + JB],
                    start=(g, d, t) == (0, 0, 0),
                    stop=(g, d, t) == (LISTS - 1, 0, PACK - 1),
                )

        first_half, second_half = range(BANKS // 2), range(BANKS // 2, BANKS)

        RAW00A, RAW00B, RAW01A, RAW01B, RAW10, ROUNDED00, ROUNDED01 = 64, 72, 78, 82, 86, 94, 102
        ROUNDED10, ROUNDED11, ROUNDED20, ROUNDED21, PLANE0, PICKED0, PARTED0 = 192, 196, 200, 204, 208, 210, 214
        RAW11, RAW20, RAW21A, RAW21B, RAW_DOWN = RAW00A, ROUNDED00, RAW01A, ROUNDED01, RAW00B
        quarter = 2 * JB

        table_words = placed("table_words", [P, T], I32, 2)
        nc.sync.dma_start(table_words[:], tab_words[0].rearrange("p t b -> p (t b)").bitcast(I32))
        load_weight(0, 0, (RAW00A, RAW00B))
        load_weight(0, 1, (RAW01A, RAW01B))
        load_weight(1, 0, (RAW10,))

        gather_scales(0, PLANE0)
        pieces = gather_pieces(0, 0, [HALF] * 2, PICKED0)
        part_pieces(0, pieces[:1], PARTED0)
        round_and_quantise(0, 0, ROUNDED00)
        part_pieces(0, pieces[1:], RAW00B + 4)
        load_weight(1, 1, (RAW11,))
        load_weight(2, 0, (RAW20,))
        for c in range(BANKS):
            first_layer(0, 0, c)

        pieces = gather_pieces(1, 0, [HALF] * 2, RAW00B)
        round_and_quantise(0, 1, ROUNDED01)
        load_weight(2, 1, (RAW21A, RAW21B))
        for c in range(BANKS):
            first_layer(0, 1, c)

        part_pieces(1, pieces, RAW01B)
        round_and_quantise(1, 0, ROUNDED10)
        raw_down = placed("raw_down", [P, PACK, N], F32, RAW_DOWN)
        down_rows = wd.rearrange("(c t u) n -> u c t n", t=PACK, u=2)
        for u in range(2):
            nc.sync.dma_start(raw_down[u:P:2], down_rows[u])
        for c in range(6):
            first_layer(1, 0, c)
        gather_scales(1, RAW10)
        for c in range(6, BANKS):
            first_layer(1, 0, c)

        round_and_quantise(1, 1, ROUNDED11)
        bias = placed("bias", [P, PRODUCTS], F32, ROUNDED10)
        nc.sync.dma_start(bias[:], b.rearrange("(p c) -> p c", p=P))
        for c in range(BANKS):
            first_layer(1, 1, c)

        pieces = gather_pieces(2, 0, [HALF], RAW11)
        gather_scales(2, RAW11 + 2)
        round_and_quantise(2, 0, ROUNDED20)
        part_pieces(2, pieces, RAW20)

        round_and_quantise(2, 1, ROUNDED21)
        pieces = gather_pieces(2, HALF, [quarter, JB, JB], RAW21B)
        for c in first_half:
            first_layer(2, 1, c)
            first_layer(2, 0, c)

        rounded_down = placed("rounded_down", [P, PACK * N], BF16, 218)
        nc.scalar.copy(
            rounded_down[:].rearrange("p (c m u t) -> p m c t u", c=PRODUCTS, u=2, t=PACK),
            raw_down[:].rearrange("p t (m u c) -> p m c t u", u=2, c=PRODUCTS),
        )
        down_codes = placed("down_codes", [P, N], U32, 143)
        down_scales = placed("down_scales", [P, N], U8, 144)
        nc.vector.quantize_mx(down_codes[:].bitcast(FP8X4), down_scales[:], rounded_down[:])

        part_pieces(2, pieces, RAW_DOWN)
        for c in second_half:
            first_layer(2, 1, c)
            first_layer(2, 0, c)

        active = []
        for c in range(BANKS):
            active.append(placed(f"active{c}", [P, JB, PACK], F32, 13 + 2 * c))
            nc.scalar.activation(active[c][:], banks[c][:].rearrange("p t j -> p j t"), ACT.Silu)

        hidden = {c0: placed(f"hidden{c0}", [P, count, JB, PACK], BF16, 150 + c0) for c0, count in GROUPS}
        sums = {}

        def smooth_bank(c0, c):
            nc.vector.tensor_tensor(hidden[c0][:, c - c0], active[c][:], smooth[:], ALU.mult)

        def second_layer(c0, count):
            hidden_codes = placed(f"hidden_codes{c0}", [P, count * JB], U32, 29 + c0 / 2)
            hidden_scales = placed(f"hidden_scales{c0}", [P, count * JB], U8, 33 + c0 / 8)
            nc.vector.quantize_mx(hidden_codes[:].bitcast(FP8X4), hidden_scales[:], hidden[c0][:].rearrange("p c j t -> p (c j t)"))
            if c0 == BANKS - 1:
                sums[c0] = [psum.tile([P, JB], F32, name=f"last_sums{n}", tag=f"bank{bank}")[:] for n, bank in enumerate((c0, 1))]
            else:
                both = psum.tile([P, PRODUCTS, count * JB], F32, name=f"sums{c0}", tag=f"bank{c0}")
                sums[c0] = [both[:, product, :] for product in range(PRODUCTS)]
            for product in range(PRODUCTS):
                nc.tensor.matmul_mx(
                    sums[c0][product],
                    lhsT=down_codes[:, product * P:(product + 1) * P].bitcast(FP8X4),
                    lhsT_scale=down_scales[:, product * P:(product + 1) * P],
                    rhs=hidden_codes[:].bitcast(FP8X4),
                    rhs_scale=hidden_scales[:],
                    start=True,
                    stop=True,
                )

        for n, (c0, count) in enumerate(GROUPS):
            smooth_bank(c0, c0)
            if n > 0:
                second_layer(*GROUPS[n - 1])
            for c in range(c0 + 1, c0 + count):
                smooth_bank(c0, c)
        second_layer(*GROUPS[-1])

        out_rows = out.rearrange("(p c) j -> p c j", p=P)
        for c0, count in GROUPS:
            result = placed(f"result{c0}", [P, PRODUCTS, count * JB], F32, 160 + c0)
            for product in range(PRODUCTS):
                if (c0, product) == (BANKS - 1, 0):
                    nc.vector.tensor_scalar_add(result[:, product, :], sums[c0][product], bias[:, product:product + 1])
                else:
                    nc.scalar.activation(result[:, product, :], sums[c0][product], ACT.Identity, bias=bias[:, product:product + 1])
            queue = nc.scalar if c0 == GROUPS[-1][0] else nc.sync
            queue.dma_start(out_rows[:, :, c0 * JB:(c0 + count) * JB], result[:])
